import numpy as np, ml_dtypes
CORES = [16,17,18,19,32,33,34,35]
N = 8
import mx_ref
BF = ml_dtypes.bfloat16
def gcols(t, e):
    v = np.concatenate([t.reshape(8, 16, -1, 4), np.zeros((8, 16, 1, 4), BF)], axis=2)
    return np.ascontiguousarray(np.stack([v[g][:, e[g]] for g in range(8)])).reshape(128, -1)
def tile(rs):
    return np.stack(rs, axis=2).reshape(128, -1).astype(BF)
def cut(t, i, w=512):
    return t[:, w * i:w * i + w]
def pick(q, e):
    c = np.concatenate([q[0].reshape(128, -1, 4), np.zeros((128, 1, 4), np.uint8)], axis=1); s = np.concatenate([q[1], np.ones((16, 1), np.uint8)], axis=1)
    return (np.ascontiguousarray(c[:, e].reshape(128, -1)), np.ascontiguousarray(s[:, e]))
def join(*qs):
    return (np.concatenate([q[0] for q in qs], axis=1), np.concatenate([q[1] for q in qs], axis=1))
def put(q, e, v):
    c, s = q[0].reshape(128, -1, 4).copy(), q[1].copy(); c[:, e] = v[0].reshape(128, -1, 4); s[:, e] = v[1]
    return (c.reshape(128, -1), s)
def pk(c, s):
    return (np.ascontiguousarray(c), mx_ref.live(s))
def emit(q):
    return q[0], q[1]
def packed(v, rng):
    q = [mx_ref.quantize(np.ascontiguousarray(v[r])) for r in range(N)]
    return np.stack([a for a, b in q]), np.stack([mx_ref.plane(b, rng) for a, b in q])
def values_of_codes():
    e, c = np.zeros((128, 128, 4), np.float32), np.zeros((128, 2, 4), np.uint8)
    e[np.arange(128), np.arange(128), 0] = 1
    c[:127, :, 0] = np.arange(256).reshape(2, 128).T[:127]
    return mx_ref.matmul(mx_ref.quantize(e.reshape(128, 512).astype(BF)), (c.reshape(128, 8), np.full((16, 2), 127, np.uint8))).T.reshape(-1).astype(np.float64)
CODE_VALUE, SCALE_VALUE = values_of_codes(), 2.0 ** (np.arange(256) - 127.0)
def decode(q):
    return (CODE_VALUE[q[0]].reshape(16, 8, -1, 4) * SCALE_VALUE[q[1]][:, None, :, None] + 0.0).reshape(128, -1).astype(np.float32)
def f(rng, *shape):
    return mx_ref.flush((rng.standard_normal(shape, dtype=np.float32) * np.exp2(rng.integers(-2, 3, shape[:-1] + (1,)))).astype(BF))
def wide(rng, *shape, cols=0):
    v = rng.standard_normal(shape, dtype=np.float32) * np.exp2(rng.integers(-12, 13, shape)).astype(np.float32)
    if cols: v *= np.repeat(np.exp2(rng.integers(-cols, cols + 1, shape[:-2] + (1, shape[-1] // 4))) * (rng.random(shape[:-2] + (1, shape[-1] // 4)) > 0.0625), 4, axis=-1).astype(np.float32)
    return mx_ref.flush(v.astype(BF))
C, H, E, R = 384, 64, 448, 3
def big(v):
    v = v.astype(np.float32)
    v[np.abs(v) < np.float32(2.0 ** -16)] = 0
    return v.astype(BF)
def numbers_of(rng):
    return {"x": big(f(rng, N, 128, 4 * C)), "u": np.array(f(rng, N, 128, 512)), "v": np.array(f(rng, N, 128, 512))}
def layers(rng):
    return big(f(rng, N, 128, 2048)).reshape(N, 8, 16, 4, 8, 16, 4)
def weights(rng, w):
    c, p = packed(np.ascontiguousarray(w).reshape(N, 128, 2048), rng)
    return {"wc": c, "ws": p}
def setup_inputs(rng):
    return {**numbers_of(rng), **weights(rng, layers(rng))}
def setup_inputs_ties(rng):
    d = numbers_of(rng)
    e = rng.permutation(N)
    x = d["x"].reshape(N, 8, 16, C, 4)
    for r in range(N):
        k = rng.permutation(C) % 3
        if r == e[0]: k = np.zeros(C, int)
        elif r in e[2::2]: k = rng.permutation(3)[np.arange(C) % 3]
        a = x[r][:, :8, :3].copy()
        a[:, :, 2] = 0
        x[r][:, :8] = a[:, :, k]
    x[e[1]] = 0
    u = d["u"].reshape(N, 8, 16, 128, 4)
    u[:, :, 8:, ::16] = 0
    u[:, :, 8:, 1::16] = 0
    w = layers(rng)
    w[:, :, :, :, :, :8] = 0
    return {"x": x.reshape(N, 128, 4 * C), "u": u.reshape(N, 128, 512), "v": d["v"], **weights(rng, w)}
def setup_inputs_near(rng):
    d = numbers_of(rng)
    x = d["x"].reshape(N, 8, 16, C, 4)
    u = d["u"].reshape(N, 128, 128, 4)
    o = rng.permutation(N) % 4
    x[:, :, :8] = 0
    u[:, :, ::16] = 0
    u[:, :, 1::16] = 0
    for r in range(N):
        s = rng.integers(-1, 2, (8, 2, C)).astype(np.float32)
        if o[r] % 2 == 1: s = s[:, :, np.arange(C) // 16]
        if o[r] < 2: s = s * np.float32(2.0 ** -29)
        for g in rng.permutation(8)[:4]: s[g, :, rng.integers(C)] = 2.0 ** 29 * rng.choice([-1.0, 1.0], 2)
        x[r, :, :2, :, 0] = s.astype(BF)
        for h in range(0, 128, 16):
            u[r, h, h, 0] = 2.0 ** -30 if o[r] < 2 else 1.0
            u[r, h + 1, h + 1, 0] = 2.0 ** -30 if o[r] < 2 else 1.0
    w = layers(rng)
    w[:, :, :8] = 0
    w[:, :, :, :, :, :8] = 0
    return {"x": x.reshape(N, 128, 4 * C), "u": u.reshape(N, 128, 512), "v": d["v"], **weights(rng, w)}
def setup_inputs_late(rng):
    d = numbers_of(rng)
    x = d["x"].reshape(N, 8, 16, C, 4)
    c = (rng.permutation(N) % 2 * 2.0 - 1.0).astype(np.float32).astype(BF)
    x[:, :, 0] = c[:, None, None, None]
    u = d["u"].reshape(N, 128, 128, 4)
    u[:, :, ::16] = 0
    u[:, :, 1::16] = 0
    for h in range(0, 128, 16):
        u[:, h, h, 0] = 1
        u[:, h, h + 1, 1] = 1
    return {"x": x.reshape(N, 128, 4 * C), "u": u.reshape(N, 128, 512), "v": d["v"], **weights(rng, layers(rng))}
def setup_inputs_huge(rng):
    d = numbers_of(rng)
    h = rng.permutation(8)
    x = -0.95 - 0.05 * rng.random((N, 8, 16, C, 4))
    x[:, h[4:]] = (0.75 + 0.1 * rng.random((N, 4, 16, C, 4))) * rng.choice([-1.0, 1.0], (N, 4, 1, C, 1))
    u = d["u"].reshape(N, 128, 128, 4)
    u[:, :, ::16] = 0
    u[:, :, 1::16] = 0
    for r in range(N):
        for g in range(8):
            for b in range(2):
                a = 16 * int(rng.choice(h[4:]))
                u[r, a:a + 16, 16 * g + b] = (2.0 ** 30 * (1 - 0.1 * rng.random((16, 4))) * rng.choice([-1.0, 1.0])).astype(np.float32).astype(BF)
    w = np.zeros((N, 128, 4, 128, 4), np.float32)
    i = np.arange(128)
    for b in range(4): w[:, i, b, i, b] = -1
    return {"x": (2.0 ** 30 * x).astype(np.float32).reshape(N, 128, 4 * C).astype(BF), "u": u.reshape(N, 128, 512), "v": d["v"], **weights(rng, w.astype(BF))}
def setup_inputs_spread(rng):
    d = setup_inputs(rng)
    d["x"] = big(wide(rng, N, 128, 4 * C, cols=6))
    return d
def check_inputs(d):
    b = []
    for k in ("x", "u", "v"):
        a = np.abs(d[k].astype(np.float32))
        if not (np.isfinite(a).all() and ((a == 0) | (a >= 2.0 ** -30) & (a <= 2.0 ** 30)).all()): b.append("a value of " + k)
    none, least, most = [emit(mx_ref.quantize(np.full((128, 16), k, np.float32).astype(BF)))[1][0, 0] for k in (0.0, 2.0 ** -30, 2.0 ** 30)]
    for r in range(N):
        if ((d["wc"][r] == 0x7F) | (d["wc"][r] == 0xFF)).any(): b.append("wc: a code that is no number")
        s = mx_ref.live(d["ws"][r])
        if ((s != none) & ((s < least) | (s > most))).any(): b.append("ws: a scale out of range")
    return b
def reference(x, u, v, wc, ws):
    qu = [mx_ref.quantize(u[r]) for r in range(N)]
    lay = [pk(wc[r], ws[r]) for r in range(N)]
    now = [x[r] for r in range(N)]
    level = np.zeros((N, 8, E), np.int64)
    for t in range(R):
        d = 2 ** t
        q = [mx_ref.quantize(now[r]) for r in range(N)]
        halo = [pick(q[r], np.arange(H)) for r in range(N)]
        came = decode(join(*halo)).astype(BF)
        made = []
        for r in range(N):
            e = (r + 1) % N
            s = mx_ref.matmul(qu[r], join(q[r], halo[e]))
            if t == 0: word = 2 * (s[::16] > 0) + (s[1::16] > 0)
            else: word = 2 * level[r] + (s[::16] > 0)
            key = 1024 * word
            key[:, :E - d] += 1 + word[:, d:]
            o = np.argsort(key, axis=1, kind="stable")
            for g in range(8): level[r, g] = np.searchsorted(key[g, o[g]], key[g])
            n, m = np.zeros((8, E), np.int64), np.zeros((8, E), np.int64)
            np.put_along_axis(n, o, np.concatenate([o[:, :1], o[:, :-1]], axis=1), axis=1)
            np.put_along_axis(m, o, np.concatenate([o[:, 1:], o[:, -1:]], axis=1), axis=1)
            a = np.concatenate([now[r], cut(came, e, 4 * H)], axis=1)
            most = np.maximum(gcols(a, n[:, :C]).astype(np.float32), gcols(a, m[:, :C]).astype(np.float32))
            z = mx_ref.quantize(((now[r].astype(np.float32) + most) * np.float32(0.5)).astype(BF))
            made.append(tile([mx_ref.matmul(pick(lay[r], np.arange(128 * b, 128 * b + 128)), z) * np.float32(0.03125) + now[r][:, b::4].astype(np.float32) for b in range(4)]))
        now = made
    y, lv = np.zeros((N, 128, C), np.float32), np.zeros((N, 8, E), np.float32)
    oc, osc = np.zeros((N, 128, 4 * C), np.uint8), np.zeros((N, 16, C), np.uint8)
    for r in range(N):
        q = mx_ref.quantize(now[r])
        y[r] = mx_ref.matmul(mx_ref.quantize(v[r]), q)
        lv[r] = level[r]
        oc[r], osc[r] = emit(q)
    return {"y": y, "lv": lv, "oc": oc, "osc": osc}

@@ -1,0 +1,380 @@
+from concourse.mybir import dt, AluOpType, ActivationFunctionType
+
+C, H, E, NR = 384, 64, 448, 3
+OFF = 16
+NS = (16, 16, 18)
+
+SCRATCH = {
+    "ut": ("sbuf", [128, 512], "bfloat16"), "vt": ("sbuf", [128, 512], "bfloat16"),
+    "qu": ("sbuf", [128, 128], "float8_e4m3fn_x4"), "su": ("sbuf", [128, 128], "uint8"),
+    "qur": ("sbuf", [128, 256], "float8_e4m3fn_x4"), "sur": ("sbuf", [128, 256], "uint8"),
+    "qv": ("sbuf", [128, 128], "float8_e4m3fn_x4"), "sv": ("sbuf", [128, 128], "uint8"),
+    "qw": ("sbuf", [128, 512], "float8_e4m3fn_x4"), "sw": ("sbuf", [128, 512], "uint8"),
+    "et": ("sbuf", [128, 2048], "bfloat16"),
+    "qe": ("sbuf", [128, 512], "float8_e4m3fn_x4"), "se": ("sbuf", [128, 512], "uint8"),
+    "zt": ("sbuf", [128, 1536], "bfloat16"),
+    "qz": ("sbuf", [128, 384], "float8_e4m3fn_x4"), "sz": ("sbuf", [128, 384], "uint8"),
+    "vp": ("sbuf", [128, 4 * E], "bfloat16"), "x32": ("sbuf", [128, 4 * C], "bfloat16"),
+    "vs": ("sbuf", [128, 4 * E], "bfloat16"), "mm": ("sbuf", [128, 4 * E], "bfloat16"),
+    "hb": ("sbuf", [128, 128], "bfloat16"), "ident": ("sbuf", [128, 128], "bfloat16"),
+    "iof": ("sbuf", [128, E], "float32"), "iom": ("sbuf", [128, E], "bfloat16"),
+    "ones": ("sbuf", [128, E], "bfloat16"),
+    "uo": ("sbuf", [128, 16], "int32"), "uo16": ("sbuf", [128, 16], "uint16"),
+    "pin": ("sbuf", [128, 1], "int32"), "pod": ("sbuf", [128, 1], "int32"), "pla": ("sbuf", [128, 1], "int32"),
+    "ev": ("sbuf", [128, 1], "float32"), "od": ("sbuf", [128, 1], "float32"), "pl": ("sbuf", [128, 1], "float32"),
+    "qrow": ("sbuf", [128, E], "float32"), "tri": ("sbuf", [128, E], "float32"),
+    "t1": ("sbuf", [128, E], "bfloat16"), "t2": ("sbuf", [128, E], "bfloat16"),
+    "w5": ("sbuf", [128, E + 16], "bfloat16"), "w6": ("sbuf", [128, E], "bfloat16"),
+    "er": ("sbuf", [128, E + 16], "float32"), "lr": ("sbuf", [128, E + 16], "float32"),
+    "ar1": ("sbuf", [128, E + 16], "bfloat16"), "ar2": ("sbuf", [128, E + 16], "bfloat16"),
+    "al": ("sbuf", [128, E], "float32"), "ag": ("sbuf", [128, E], "float32"),
+    "g1": ("sbuf", [128, E], "float32"), "s1": ("sbuf", [128, E], "float32"), "s2": ("sbuf", [128, E], "float32"),
+    "kr": ("sbuf", [128, E + 32], "float32"), "ka": ("sbuf", [128, E], "float32"), "kb": ("sbuf", [128, E + 32], "float32"),
+    "o1": ("sbuf", [128, 28], "float32"), "o2": ("sbuf", [128, 28], "float32"), "own": ("sbuf", [128, 28], "float32"),
+    "junk": ("sbuf", [128, 4 * E], "bfloat16"), "acc": ("sbuf", [128, 28], "float32"),
+    "cb": ("sbuf", [128, 12 * E], "bfloat16"), "sc": ("sbuf", [128, 6 * E], "float32"),
+    "i1": ("sbuf", [128, 8], "int32"), "i2": ("sbuf", [128, 16], "int32"),
+    "posf": ("sbuf", [128, 28], "float32"), "pos": ("sbuf", [128, 28], "uint16"),
+    "ordr": ("sbuf", [128, E + 32], "bfloat16"), "oa": ("sbuf", [128, E], "bfloat16"), "ob": ("sbuf", [128, E + 32], "bfloat16"),
+    "p1": ("sbuf", [128, 28], "bfloat16"), "p2": ("sbuf", [128, 28], "bfloat16"), "p3": ("sbuf", [128, 28], "bfloat16"),
+    "ordl": ("sbuf", [128, 28], "uint16"),
+    "dd": ("sbuf", [128, 2 * E], "float32"), "kt": ("sbuf", [128, E], "float32"),
+    "eq": ("sbuf", [128, E], "bfloat16"), "f1": ("sbuf", [128, 224], "bfloat16"), "f2": ("sbuf", [128, 112], "bfloat16"),
+    "f3": ("sbuf", [128, 56], "bfloat16"), "f4": ("sbuf", [128, 28], "float32"),
+    "ks": ("sbuf", [128, E + 16], "float32"), "eqs": ("sbuf", [128, E], "bfloat16"), "rr": ("sbuf", [128, E], "float32"),
+    "lw": ("sbuf", [128, E], "float32"), "lvr": ("sbuf", [128, E], "float32"), "yr": ("sbuf", [128, C], "float32"),
+    "ps": ("psum", [128, 4096], "float32"),
+}
+for _t in range(NR + 1):
+    SCRATCH["xt%d" % _t] = ("sbuf", [128, 4 * C], "bfloat16")
+    SCRATCH["qx%d" % _t] = ("sbuf", [128, E], "float8_e4m3fn_x4")
+    SCRATCH["sx%d" % _t] = ("sbuf", [128, E], "uint8")
+DMAS = ["dxa", "dxb", "du", "dv", "dwc", "dws", "dlv", "dya", "dyb", "dca", "dcb"] + ["ds%d" % k for k in range(4)]
+SEMAPHORES = ["vec", "act", "ten", "pool", "left"] + ["arr%d" % t for t in range(NR)] + DMAS
+
+ADD, SUB, MUL, MAX = AluOpType.add, AluOpType.subtract, AluOpType.mult, AluOpType.max
+GT, LT, LE, EQ = AluOpType.is_gt, AluOpType.is_lt, AluOpType.is_le, AluOpType.is_equal
+COPY, IDEN, SIGN = ActivationFunctionType.Copy, ActivationFunctionType.Identity, ActivationFunctionType.Sign
+CENTER = 5380840.0
+
+
+def rank_program(g, core, T, topo):
+    rank = T.rank_of(core)
+    if rank is None:
+        return
+    n = len(T.cores)
+    prev, nxt = T.cores[(rank - 1) % n], T.cores[(rank + 1) % n]
+
+    def send_engines(src, dst):
+        return topo.engines(src, dst)[:8]
+
+    queue = {"v": g.vector, "a": g.scalar, "t": g.tensor, "g": g, "s": g.sync}
+    semof = {"v": "vec", "a": "act", "t": "ten", "g": "pool"}
+    count = {"vec": 0, "act": 0, "ten": 0, "pool": 0}
+    seen = {q: {} for q in queue}
+    hist = {}
+
+    def waits(q, reads, writes):
+        need = {}
+        for regs, isw in ((reads, False), (writes, True)):
+            for name, lo, hi in regs:
+                for l, h, w, oq, sem, val in hist.get(name, ()):
+                    if l < hi and lo < h and (w or isw):
+                        if oq == q and isw and not w:
+                            continue
+                        need[sem] = max(need.get(sem, 0), val)
+        for sem in sorted(need):
+            if seen[q].get(sem, 0) < need[sem]:
+                queue[q].wait_ge(T.sem[sem], need[sem])
+                seen[q][sem] = need[sem]
+
+    def note(q, reads, writes, sem, val):
+        for name, lo, hi in writes:
+            hist[name] = [e for e in hist.get(name, ()) if not (lo <= e[0] and e[1] <= hi)] + [(lo, hi, True, q, sem, val)]
+        for name, lo, hi in reads:
+            hist.setdefault(name, []).append((lo, hi, False, q, sem, val))
+
+    def op(q, reads, writes, fn, *args, **kw):
+        waits(q, reads, writes)
+        sem = semof[q]
+        fn(*args, **kw).then_inc(T.sem[sem], 1)
+        count[sem] += 1
+        note(q, reads, writes, sem, count[sem])
+
+    def dma(q, sem, reads, writes, out, in_):
+        waits(q, reads, writes)
+        queue[q].dma_start(out, in_).then_inc(T.sem[sem], 16)
+        note("dma", reads, writes, sem, 16)
+
+    def V(name, lo, hi, step=1):
+        return T[name][:, lo:hi] if step == 1 else T[name][:, lo:hi:step]
+
+    def tt(out, a, b, o, R, W):
+        op("v", R, W, g.vector.tensor_tensor, out, a, b, o)
+
+    def ts(out, a, s1, s2, o0, o1, R, W):
+        if o1 is None:
+            op("v", R, W, g.vector.tensor_scalar, out, a, s1, None, o0)
+        else:
+            op("v", R, W, g.vector.tensor_scalar, out, a, s1, s2, o0, o1)
+
+    def tc(out, in_, R, W):
+        op("v", R, W, g.vector.tensor_copy, out, in_)
+
+    def act(out, in_, f, R, W, **kw):
+        op("a", R, W, g.scalar.activation, out, in_, f, **kw)
+
+    def fill(name, lo, hi, c):
+        op("v", [], [(name, lo, hi)], g.vector.memset, V(name, lo, hi), c)
+
+    def quant(codes, plane, src, lo, hi, R):
+        op("v", R, [(codes, lo, hi)], g.vector.quantize_mx, V(codes, lo, hi), V(plane, lo, hi), V(src, 4 * lo, 4 * hi))
+
+    def mx(bank, cols, l, ls, llo, r, rs, rlo, rhi):
+        op("t", [(l, llo, llo + 128), (r, rlo, rhi)], [("b%d" % bank, 0, 1)], g.tensor.matmul_mx,
+           T.ps[:, 512 * bank:512 * bank + cols], V(l, llo, llo + 128), V(ls, llo, llo + 128),
+           V(r, rlo, rhi), V(rs, rlo, rhi), True, True)
+
+    def bank(k, lo, hi):
+        return T.ps[:, 512 * k + lo:512 * k + hi]
+
+    def send(t):
+        waits("g", [("qx%d" % t, 0, H)], [])
+        rid, pid = topo.addr(prev)[0], topo.addr(prev)[1]
+        m = 0
+        for e in send_engines(core, prev):
+            m |= 1 << e
+        q, s = "qx%d" % t, "sx%d" % t
+        g.remote_dma(V(q, C, E).bitcast(dt.uint8), V(q, 0, H).bitcast(dt.uint8), T.sem["arr%d" % t], T.sem.left, pid, rid, m)
+        g.remote_dma(V(s, C, E), V(s, 0, H), T.sem["arr%d" % t], T.sem.left, pid, rid, m)
+        note("remote", [], [(q, C, E)], "arr%d" % t, 2 * len(send_engines(nxt, core)))
+
+    xr = lambda t, lo, hi: [("x%d_%d" % (t, b), lo, hi) for b in range(4)]
+    dma("s", "dxa", [], xr(0, 0, 128), T.xt0[:, 0:512], T.x[:, 0:512])
+    dma("a", "du", [], [("ut", 0, 128)], T.ut[:, :], T.u[:, :])
+    dma("s", "dxb", [], xr(0, 128, C), T.xt0[:, 512:1536], T.x[:, 512:1536])
+    dma("s", "dwc", [], [("qw", 0, 512)], T.qw[:, 0:512].bitcast(dt.uint8), T.wc[:, :])
+    dma("s", "dws", [], [("qw", 0, 512)], T.sw[:, :], T.ws[:, :])
+    dma("a", "dv", [], [("vt", 0, 128)], T.vt[:, :], T.v[:, :])
+    hist["qw"] = [(0, 512, True, "dma", "dwc", 16), (0, 512, True, "dma", "dws", 16)]
+    fill("hb", 0, 128, 0.5)
+    op("g", [], [("uo", 0, 16)], g.iota, T.uo[:, :], [[1, 2], [16, 8]], 0, 0)
+    op("g", [], [("pin", 0, 1)], g.iota, T.pin[:, :], [[0, 1]], 0, 1)
+    op("g", [("hb", 0, 128)], [("ident", 0, 128)], g.affine_select, T.ident[:, :], T.hb[:, :], [[-1, 128]], EQ, 0.0, 0, 1)
+    op("g", [], [("iof", 0, E)], g.iota, T.iof[:, :], [[1, E]], 0, 0, allow_small_or_imprecise_dtypes=True)
+    fill("et", 0, 2048, 0.0)
+    tc(T.uo16[:, :], T.uo[:, :], [("uo", 0, 16)], [("uo16", 0, 16)])
+    op("v", [("pin", 0, 1)], [("pod", 0, 1)], g.vector.tensor_scalar, T.pod[:, :], T.pin[:, :], 4, 1, AluOpType.logical_shift_right, AluOpType.bitwise_and)
+    op("v", [("pin", 0, 1)], [("pla", 0, 1)], g.vector.tensor_scalar, T.pla[:, :], T.pin[:, :], 15, None, AluOpType.bitwise_and)
+    tc(T.od[:, :], T.pod[:, :], [("pod", 0, 1)], [("od", 0, 1)])
+    tc(T.pl[:, :], T.pla[:, :], [("pla", 0, 1)], [("pl", 0, 1)])
+    ts(T.ev[:, :], T.od[:, :], -1.0, 1.0, MUL, ADD, [("od", 0, 1)], [("ev", 0, 1)])
+    fill("w5", E, E + 16, -512.0)
+    fill("er", E, E + 16, -256.0)
+    fill("lr", E, E + 16, -256.0)
+    fill("ar1", E, E + 16, 0.0)
+    fill("ar2", E, E + 16, 0.0)
+    for nm in ("kr", "ordr"):
+        fill(nm, 0, OFF, 0.0)
+        fill(nm, OFF + E, E + 32, 0.0)
+    fill("ones", 0, E, 1.0)
+    fill("eq", 0, 28, 0.0)
+    fill("ks", 0, 8, -9.0e6)
+    for b in range(4):
+        tc(T.et[:, 512 * b + b:512 * b + 512:4], T.ident[:, :], [("ident", 0, 128)], [("et", 512 * b, 512 * b + 512)])
+    quant("qx0", "sx0", "xt0", 0, 128, xr(0, 0, 128))
+    send(0)
+    quant("qu", "su", "ut", 0, 128, [("ut", 0, 128)])
+    op("v", [("qu", 0, 128), ("uo16", 0, 16)], [("qur", 0, 256)], g.vector.tensor_copy,
+       T.qur[:, 0:256].bitcast(dt.uint32), T.qu[:, 0:128].bitcast(dt.uint32).indirect(T.uo16[:, 0:16]))
+    op("a", [("qu", 0, 128), ("uo16", 0, 16)], [("qurs", 0, 256)], g.scalar.activation,
+       T.sur[:, 0:256], T.su[:, 0:128].indirect(T.uo16[:, 0:16]), COPY)
+    quant("qx0", "sx0", "xt0", 128, C, xr(0, 128, C))
+    quant("qe", "se", "et", 0, 512, [("et", 0, 2048)])
+    ts(T.iom[:, :], T.iof[:, :], -192.0, None, ADD, None, [("iof", 0, E)], [("iom", 0, E)])
+    quant("qv", "sv", "vt", 0, 128, [("vt", 0, 128)])
+    op("g", [], [("qrow", 0, E)], g.iota, T.qrow[:, :], [[0, 28], [1, 16]], 0, 0, allow_small_or_imprecise_dtypes=True)
+    for b in range(4):
+        act(V("vp", E * b, E * b + C), V("xt0", b, 4 * C, 4), COPY, [("x0_%d" % b, 0, C)], [("vp%d" % b, 0, C)], scale=0.5)
+    waits("t", [("qurs", 0, 256)], [])
+
+    def wrap(src, ta, tb, a1, a2, out, dtype_tag):
+        op("v", [(src, OFF, OFF + E)], [(ta, 0, E)], g.vector.transpose, V(ta, 0, E), V(src, OFF, OFF + E))
+        op("v", [(src, 0, E + 32)], [(tb, 0, E)], g.vector.transpose, V(tb, 0, E + 32), V(src, 0, E + 32))
+        A, B = [(ta, 0, E)], [(tb, 0, E)]
+        ts(V(a1, 0, 28, 2), V(ta, 0, E, 32), T.ev[:, 0:1], None, MUL, None, A + [("ev", 0, 1)], [(a1 + "e", 0, 1)])
+        ts(V(a2, 1, 28, 2), V(ta, 16, E, 32), T.od[:, 0:1], None, MUL, None, A + [("od", 0, 1)], [(a2 + "o", 0, 1)])
+        ts(V(a2, 0, 28, 2), V(tb, 16, E, 32), T.od[:, 0:1], None, MUL, None, B, [(a2 + "e", 0, 1)])
+        ts(V(a1, 1, 28, 2), V(tb, 32, E + 32, 32), T.ev[:, 0:1], None, MUL, None, B, [(a1 + "o", 0, 1)])
+        tt(V(out, 0, 28), V(a1, 0, 28), V(a2, 0, 28), ADD,
+           [(a1 + "e", 0, 1), (a2 + "o", 0, 1), (a2 + "e", 0, 1), (a1 + "o", 0, 1)], [(out, 0, 28)])
+
+    for t in range(NR):
+        d = 2 ** t
+        qx, sx = "qx%d" % t, "sx%d" % t
+        mx(0, E, "qur", "sur", 0, qx, sx, 0, E)
+        if t == 0:
+            mx(1, E, "qur", "sur", 128, qx, sx, 0, E)
+        for b in range(4):
+            mx(4 + b, 128, "qe", "se", 128 * b, qx, sx, E - 128, E)
+        K = V("kr", OFF, OFF + E)
+        KR = [("kr", OFF, OFF + E)]
+        if t == 0:
+            ts(V("t1", 0, E), bank(0, 0, E), 0.0, 1024.0, GT, MUL, [("b0", 0, 1)], [("t1", 0, E)])
+            ts(V("t2", 0, E), bank(1, 0, E), 0.0, 512.0, GT, MUL, [("b1", 0, 1)], [("t2", 0, E)])
+            tt(V("w5", 0, E), V("t1", 0, E), V("t2", 0, E), ADD, [("t1", 0, E), ("t2", 0, E)], [("w5", 0, E)])
+            ts(V("w6", 0, E), V("w5", 0, E), 5.0, 512.0, MUL, ADD, [("w5", 0, E)], [("w6", 0, E)])
+            tt(V("er", 0, E), V("w6", 0, E), V("w5", 1, E + 1), ADD, [("w6", 0, E), ("w5", 0, E + 16)], [("er", 0, E)])
+            tt(K, V("er", 0, E), V("iof", 0, E), ADD, [("er", 0, E), ("iof", 0, E)], KR)
+        else:
+            ar = "ar%d" % t
+            unit, fac = ((512.0, 41.0), (1.0, 3281.0))[t - 1]
+            ts(V(ar, 0, E), bank(0, 0, E), 0.0, unit, GT, MUL, [("b0", 0, 1)], [(ar, 0, E)])
+            ts(V("al", 0, E), V(ar, 0, E), fac, None, MUL, None, [(ar, 0, E)], [("al", 0, E)])
+            tt(V("ag", 0, E), V("al", 0, E), V("g1", 0, E), ADD, [("al", 0, E), ("g1", 0, E)], [("ag", 0, E)])
+            tt(K, V("ag", 0, E), V(ar, d, E + d), ADD, [("ag", 0, E), (ar, 0, E + 16)], KR)
+        for b in range(4):
+            act(V("vp", E * b + C, E * b + E), bank(4 + b, 64, 128), COPY, [("b%d" % (4 + b), 0, 1)], [("vp%d" % b, C, E)])
+        last = t == NR - 1
+        if last:
+            act(V("dd", E, 2 * E), K, IDEN, KR, [("dd", E, 2 * E)], bias=-0.5)
+            act(V("dd", 0, E), K, IDEN, KR, [("dd", 0, E)], bias=0.5)
+        wrap("kr", "ka", "kb", "o1", "o2", "own", "f")
+        ns = NS[t]
+        nv = 28 - ns
+        half = nv // 2
+
+        def row(c):
+            if last:
+                return V("dd", 16 * c + 16, 16 * c + 16 + E), [("dd", 16 * c + 16, 16 * c + 16 + E)]
+            return K, KR
+
+        for c in range(ns):
+            v, r = row(c)
+            j = c % 4
+            act(V("junk", E * j, E * j + E), v, SIGN, r + [("own", 0, 28)], [("junk%d" % j, 0, 1), ("acc", c, c + 1)],
+                bias=T.own[:, c:c + 1], scale=-1.0, accum_out=T.acc[:, c:c + 1])
+        for k in range(nv):
+            v, r = row(ns + k)
+            o = [("cb", k, k + 1)]
+            if k < half:
+                ts(V("cb", E * k, E * k + E), v, T.own[:, ns + k:ns + k + 1], None, LT, None, r + [("own", 0, 28)], o)
+            else:
+                ts(V("cb", E * k, E * k + E), v, T.own[:, ns + k:ns + k + 1], 1024.0, LT, MUL, r + [("own", 0, 28)], o)
+        for k in range(half):
+            op("v", [("cb", k, k + 1), ("cb", half + k, half + k + 1)], [("sc", k, k + 1)], g.vector.tensor_tensor_scan,
+               V("sc", E * k, E * k + E), V("cb", E * k, E * k + E), V("cb", E * (half + k), E * (half + k) + E), 0.0, ADD, ADD)
+        if last:
+            tt(V("kt", 0, E), K, V("tri", 0, E), ADD, KR + [("tri", 0, E)], [("kt", 0, E)])
+            for q in range(1, 16):
+                tt(V("eq", 28 * q, 28 * q + 28), V("kt", q, E, 16), V("own", 0, 28), EQ, [("kt", 0, E), ("own", 0, 28)], [("eq", 28 * q, 28 * q + 28)])
+            tt(V("f1", 0, 224), V("eq", 0, 224), V("eq", 224, 448), ADD, [("eq", 0, 448)], [("f1", 0, 1)])
+            tt(V("f2", 0, 112), V("f1", 0, 112), V("f1", 112, 224), ADD, [("f1", 0, 1)], [("f2", 0, 1)])
+            tt(V("f3", 0, 56), V("f2", 0, 56), V("f2", 56, 112), ADD, [("f2", 0, 1)], [("f3", 0, 1)])
+            tt(V("f4", 0, 28), V("f3", 0, 28), V("f3", 28, 56), ADD, [("f3", 0, 1)], [("f4", 0, 1)])
+        tc(V("i1", 0, half), V("sc", E - 1, E * half, E), [("sc", 0, half)], [("i1", 0, 1)])
+        op("v", [("i1", 0, 1)], [("i2", 0, 1)], g.vector.tensor_scalar, V("i2", 0, half), V("i1", 0, half), 1023, None, AluOpType.bitwise_and)
+        op("v", [("i1", 0, 1)], [("i2", 1, 2)], g.vector.tensor_scalar, V("i2", half, nv), V("i1", 0, half), 10, None, AluOpType.logical_shift_right)
+        if not last:
+            tc(V("pos", ns, 28), V("i2", 0, nv), [("i2", 0, 2)], [("pos", ns, 28)])
+            ts(V("pos", 0, ns), V("acc", 0, ns), 0.5, 223.5, MUL, ADD, [("acc", 0, ns)], [("pos", 0, ns)])
+        else:
+            ts(V("posf", ns, 28), V("i2", 0, nv), -1.0, None, ADD, None, [("i2", 0, 2)], [("posf", ns, 28)])
+            ts(V("posf", 0, ns), V("acc", 0, ns), 0.5, 223.0, MUL, ADD, [("acc", 0, ns)], [("posf", 0, ns)])
+            tt(V("f4", 0, 28), V("posf", 0, 28), V("f4", 0, 28), SUB, [("posf", 0, 28), ("f4", 0, 1)], [("f4", 0, 1)])
+            tc(V("pos", 0, 28), V("f4", 0, 28), [("f4", 0, 1)], [("pos", 0, 28)])
+        tc(V("ordr", OFF, OFF + E).indirect(V("pos", 0, 28)), V("iom", 0, E), [("iom", 0, E), ("pos", 0, 28)], [("ordr", OFF, OFF + E)])
+        wrap("ordr", "oa", "ob", "p1", "p2", "p3", "b")
+        ts(V("ordl", 0, 28), V("p3", 0, 28), 192.0, None, ADD, None, [("p3", 0, 28)], [("ordl", 0, 28)])
+        for b in range(4):
+            act(V("vs", E * b, E * b + E), V("vp", E * b, E * b + E).indirect(V("ordl", 0, 28)), COPY,
+                [("vp%d" % b, 0, E), ("ordl", 0, 28)], [("vs%d" % b, 0, 1)])
+        if last:
+            act(V("ks", 1, 1 + E), V("kr", OFF, OFF + E).indirect(V("ordl", 0, 28)), COPY, KR + [("ordl", 0, 28)], [("ks", 1, 1 + E)])
+        if t == 0:
+            for b in range(4):
+                act(V("x32", C * b, C * b + C), V("xt0", b, 4 * C, 4), COPY, [("x0_%d" % b, 0, C)], [("x32_%d" % b, 0, C)], scale=32.0)
+            act(V("s1", 0, E), V("er", 0, E), IDEN, [("er", 0, E)], [("s1", 0, E)], bias=512.0, scale=82.0)
+            act(V("s2", 0, E), V("er", 2, E + 2), COPY, [("er", 0, E + 16)], [("s2", 0, E)], scale=2.0)
+        for b in range(4):
+            o = E * b
+            tt(V("mm", o + 1, o + E - 1), V("vs", o, o + E - 2), V("vs", o + 2, o + E), MAX, [("vs%d" % b, 0, 1)], [("mm%d" % b, 0, 1)])
+            tt(V("mm", o, o + E, E - 1), V("vs", o, o + E, E - 1), V("vs", o + 1, o + E - 1, E - 3), MAX, [("vs%d" % b, 0, 1)], [("mm%d" % b, 1, 2)])
+
+        def fused(b, lo, hi):
+            tt(V("zt", 4 * lo + b, 4 * hi, 4), V("mm", E * b, E * b + E).indirect(V("pos", lo // 16, hi // 16)), V("vp", E * b + lo, E * b + hi), ADD,
+               [("mm%d" % b, 0, 2), ("pos", 0, 28), ("vp%d" % b, lo, hi)], [("z%d" % b, lo, hi)])
+
+        def product(lo, hi, b0):
+            quant("qz", "sz", "zt", lo, hi, [("z%d" % b, lo, hi) for b in range(4)])
+            for b in range(4):
+                mx(b0 + b, hi - lo, "qw", "sw", 128 * b, "qz", "sz", lo, hi)
+
+        xn = "xt%d" % (t + 1)
+
+        def update(lo, hi, b0):
+            for b in range(4):
+                r = [("x32_%d" % b, lo, hi)]
+                tt(V("x32", C * b + lo, C * b + hi), bank(b0 + b, 0, hi - lo), V("x32", C * b + lo, C * b + hi), ADD, [("b%d" % (b0 + b), 0, 1)] + r, r)
+            for b in range(4):
+                o, i, W = V(xn, 4 * lo + b, 4 * hi, 4), V("x32", C * b + lo, C * b + hi), [("x%d_%d" % (t + 1, b), lo, hi)]
+                if b < 3:
+                    act(o, i, COPY, [("x32_%d" % b, lo, hi)], W, scale=0.03125)
+                else:
+                    ts(o, i, 0.03125, None, MUL, None, [("x32_%d" % b, lo, hi)], W)
+
+        def planes(lo, hi):
+            for b in range(4):
+                act(V("vp", E * b + lo, E * b + hi), V("x32", C * b + lo, C * b + hi), COPY, [("x32_%d" % b, lo, hi)], [("vp%d" % b, lo, hi)], scale=2.0 ** -6)
+
+        qn, sn = "qx%d" % (t + 1), "sx%d" % (t + 1)
+        for b in range(4):
+            fused(b, 0, 128)
+        product(0, 128, 0)
+        fused(0, 128, C)
+        update(0, 128, 0)
+        fused(1, 128, C)
+        quant(qn, sn, xn, 0, 128, xr(t + 1, 0, 128))
+        if not last:
+            send(t + 1)
+            planes(0, 128)
+        else:
+            dma("s", "dca", [(qn, 0, 128)], [], T.oc[:, 0:512], V(qn, 0, 128).bitcast(dt.uint8))
+        fused(2, 128, C)
+        fused(3, 128, C)
+        product(128, C, 4)
+        if t == 0:
+            tt(V("g1", 0, E), V("s1", 0, E), V("s2", 0, E), ADD, [("s1", 0, E), ("s2", 0, E)], [("g1", 0, E)])
+            tt(V("g1", 0, E), V("g1", 0, E), V("iof", 0, E), ADD, [("g1", 0, E), ("iof", 0, E)], [("g1", 0, E)])
+        elif t == 1:
+            tt(V("lr", 0, E), K, V("iof", 0, E), SUB, KR + [("iof", 0, E)], [("lr", 0, E)])
+            act(V("s1", 0, E), V("lr", 0, E), IDEN, [("lr", 0, E)], [("s1", 0, E)], bias=1.0 - CENTER, scale=6562.0 / 512.0)
+            act(V("s2", 0, E), V("lr", 4, E + 4), COPY, [("lr", 0, E + 16)], [("s2", 0, E)], scale=1.0 / 256.0)
+        else:
+            tt(V("eqs", 0, E), V("ks", 1, E + 1), V("ks", 0, E), EQ, [("ks", 0, E + 1)], [("eqs", 0, E)])
+            op("v", [("ones", 0, E), ("eqs", 0, E)], [("rr", 0, E)], g.vector.tensor_tensor_scan, V("rr", 0, E), V("ones", 0, E), V("eqs", 0, E), 0.0, ADD, MUL)
+            tt(V("lw", 0, E), V("iof", 0, E), V("rr", 0, E), SUB, [("iof", 0, E), ("rr", 0, E)], [("lw", 0, E)])
+        update(128, C, 4)
+        quant(qn, sn, xn, 128, C, xr(t + 1, 128, C))
+        if t == 0:
+            ts(V("tri", 0, E), V("qrow", 0, E), T.pl[:, 0:1], 16777216.0, LE, MUL, [("qrow", 0, E), ("pl", 0, 1)], [("tri", 0, E)])
+        if t == 1:
+            tt(V("g1", 0, E), V("s1", 0, E), V("s2", 0, E), ADD, [("s1", 0, E), ("s2", 0, E)], [("g1", 0, E)])
+        if not last:
+            planes(128, C)
+
+    q, s = "qx%d" % NR, "sx%d" % NR
+    mx(0, C, "qv", "sv", 0, q, s, 0, C)
+    dma("s", "dcb", [(q, 128, C)], [], T.oc[:, 512:1536], V(q, 128, C).bitcast(dt.uint8))
+    act(V("lvr", 0, E), V("lw", 0, E).indirect(V("pos", 0, 28)), COPY, [("lw", 0, E), ("pos", 0, 28)], [("lvr", 0, E)])
+    tc(T.yr[:, :], bank(0, 0, C), [("b0", 0, 1)], [("yr", 0, C)])
+    dma("a", "dya", [("yr", 0, C)], [], T.y[:, :], T.yr[:, :])
+    for k in range(4):
+        dma("s", "ds%d" % k, [(q, 0, C)], [], T.osc[4 * k:4 * k + 4, 0:C], T[s][32 * k:32 * k + 4, 0:C])
+    dma("s", "dlv", [("lvr", 0, E)], [], T.lv[:, :], T.lvr[0:128:16, 0:E])
+    for sem in count:
+        g.wait_ge(T.sem[sem], count[sem])
+    for sem in DMAS:
+        if sem != "dyb":
+            g.wait_ge(T.sem[sem], 16)
+    g.wait_ge(T.sem.left, 2 * NR * len(send_engines(core, prev)))

@@ -2,49 +2,28 @@ from concourse.mybir import dt, AluOpType, ActivationFunctionType
 
 C, H, E, NR = 384, 64, 448, 3
 OFF = 16
-NS = (16, 16, 18)
+NS = (0, 16, 18)
 
-SCRATCH = {
-    "ut": ("sbuf", [128, 512], "bfloat16"), "vt": ("sbuf", [128, 512], "bfloat16"),
-    "qu": ("sbuf", [128, 128], "float8_e4m3fn_x4"), "su": ("sbuf", [128, 128], "uint8"),
-    "qur": ("sbuf", [128, 256], "float8_e4m3fn_x4"), "sur": ("sbuf", [128, 256], "uint8"),
-    "qv": ("sbuf", [128, 128], "float8_e4m3fn_x4"), "sv": ("sbuf", [128, 128], "uint8"),
-    "qw": ("sbuf", [128, 512], "float8_e4m3fn_x4"), "sw": ("sbuf", [128, 512], "uint8"),
-    "et": ("sbuf", [128, 2048], "bfloat16"),
-    "qe": ("sbuf", [128, 512], "float8_e4m3fn_x4"), "se": ("sbuf", [128, 512], "uint8"),
-    "zt": ("sbuf", [128, 1536], "bfloat16"),
-    "qz": ("sbuf", [128, 384], "float8_e4m3fn_x4"), "sz": ("sbuf", [128, 384], "uint8"),
-    "vp": ("sbuf", [128, 4 * E], "bfloat16"), "x32": ("sbuf", [128, 4 * C], "bfloat16"),
-    "vs": ("sbuf", [128, 4 * E], "bfloat16"), "mm": ("sbuf", [128, 4 * E], "bfloat16"),
-    "hb": ("sbuf", [128, 128], "bfloat16"), "ident": ("sbuf", [128, 128], "bfloat16"),
-    "iof": ("sbuf", [128, E], "float32"), "iom": ("sbuf", [128, E], "bfloat16"),
-    "ones": ("sbuf", [128, E], "bfloat16"),
-    "uo": ("sbuf", [128, 16], "int32"), "uo16": ("sbuf", [128, 16], "uint16"),
-    "pin": ("sbuf", [128, 1], "int32"), "pod": ("sbuf", [128, 1], "int32"), "pla": ("sbuf", [128, 1], "int32"),
-    "ev": ("sbuf", [128, 1], "float32"), "od": ("sbuf", [128, 1], "float32"), "pl": ("sbuf", [128, 1], "float32"),
-    "qrow": ("sbuf", [128, E], "float32"), "tri": ("sbuf", [128, E], "float32"),
-    "t1": ("sbuf", [128, E], "bfloat16"), "t2": ("sbuf", [128, E], "bfloat16"),
-    "w5": ("sbuf", [128, E + 16], "bfloat16"), "w6": ("sbuf", [128, E], "bfloat16"),
-    "er": ("sbuf", [128, E + 16], "float32"), "lr": ("sbuf", [128, E + 16], "float32"),
-    "ar1": ("sbuf", [128, E + 16], "bfloat16"), "ar2": ("sbuf", [128, E + 16], "bfloat16"),
-    "al": ("sbuf", [128, E], "float32"), "ag": ("sbuf", [128, E], "float32"),
-    "g1": ("sbuf", [128, E], "float32"), "s1": ("sbuf", [128, E], "float32"), "s2": ("sbuf", [128, E], "float32"),
-    "kr": ("sbuf", [128, E + 32], "float32"), "ka": ("sbuf", [128, E], "float32"), "kb": ("sbuf", [128, E + 32], "float32"),
-    "o1": ("sbuf", [128, 28], "float32"), "o2": ("sbuf", [128, 28], "float32"), "own": ("sbuf", [128, 28], "float32"),
-    "junk": ("sbuf", [128, 4 * E], "bfloat16"), "acc": ("sbuf", [128, 28], "float32"),
-    "cb": ("sbuf", [128, 12 * E], "bfloat16"), "sc": ("sbuf", [128, 6 * E], "float32"),
-    "i1": ("sbuf", [128, 8], "int32"), "i2": ("sbuf", [128, 16], "int32"),
-    "posf": ("sbuf", [128, 28], "float32"), "pos": ("sbuf", [128, 28], "uint16"),
-    "ordr": ("sbuf", [128, E + 32], "bfloat16"), "oa": ("sbuf", [128, E], "bfloat16"), "ob": ("sbuf", [128, E + 32], "bfloat16"),
-    "p1": ("sbuf", [128, 28], "bfloat16"), "p2": ("sbuf", [128, 28], "bfloat16"), "p3": ("sbuf", [128, 28], "bfloat16"),
-    "ordl": ("sbuf", [128, 28], "uint16"),
-    "dd": ("sbuf", [128, 2 * E], "float32"), "kt": ("sbuf", [128, E], "float32"),
-    "eq": ("sbuf", [128, E], "bfloat16"), "f1": ("sbuf", [128, 224], "bfloat16"), "f2": ("sbuf", [128, 112], "bfloat16"),
-    "f3": ("sbuf", [128, 56], "bfloat16"), "f4": ("sbuf", [128, 28], "float32"),
-    "ks": ("sbuf", [128, E + 16], "float32"), "eqs": ("sbuf", [128, E], "bfloat16"), "rr": ("sbuf", [128, E], "float32"),
-    "lw": ("sbuf", [128, E], "float32"), "lvr": ("sbuf", [128, E], "float32"), "yr": ("sbuf", [128, C], "float32"),
-    "ps": ("psum", [128, 4096], "float32"),
-}
+SCRATCH = {}
+for _k, _n in (("qu", 128), ("qur", 256), ("qv", 128), ("qw", 512), ("qe", 512), ("qc", 512), ("qz", C), ("qq", 212), ("qg", 128), ("qh", E + 32)):
+    SCRATCH[_k] = ("sbuf", [128, _n], "float8_e4m3fn_x4")
+    SCRATCH[{"qc": "cs"}.get(_k, "s" + _k[1:])] = ("sbuf", [128, _n], "uint8")
+for _k, _n in (("ut", 512), ("vt", 512), ("et", 2048), ("ct", 2048), ("gt", 512), ("ga", 512), ("hl", 4 * (E + 32)), ("zt", 4 * C), ("vp", 4 * E),
+               ("x32", 4 * C), ("vs", 4 * E), ("mm", 4 * E), ("hb", 128), ("ident", 128), ("iom", E), ("ones", 512), ("t1", E), ("t2", E),
+               ("w5", E + 16), ("w6", E), ("er", E + 16), ("ar1", E + 16), ("ar2", E + 16), ("junk", 4 * E), ("cb", 16 * E), ("sc", 8 * E),
+               ("ordr", E + 32), ("oa", E), ("ob", E + 32), ("eq", 848), ("eqs", E)):
+    SCRATCH[_k] = ("sbuf", [128, _n], "bfloat16")
+for _k, _n in (("iof", E), ("ev", 1), ("od", 1), ("pl", 1), ("pq", 1), ("lama", 1), ("lam", 1), ("lamb", 1), ("lams", 1), ("first", 1),
+               ("qi", 16), ("behind", 16), ("lr", E + 16), ("al", E), ("ag", E), ("g1", E),
+               ("s1", E), ("s2", E), ("kr", E + 32), ("ka", E), ("kb", E + 32), ("ma", 28), ("mb", 28), ("o1", 28), ("o2", 28),
+               ("own", 28), ("acc", 28), ("posf", 28), ("posg", 28), ("p3", 28), ("d2", 2 * E), ("ks", E + 16), ("rr", E), ("lw", E),
+               ("lvr", E), ("yr", C)):
+    SCRATCH[_k] = ("sbuf", [128, _n], "float32")
+for _k, _n in (("uo", 16), ("pin", 1), ("pod", 1), ("pla", 1), ("plq", 1)):
+    SCRATCH[_k] = ("sbuf", [128, _n], "int32")
+for _k, _n in (("uo16", 16), ("pos", 28), ("ordl", 28)):
+    SCRATCH[_k] = ("sbuf", [128, _n], "uint16")
+SCRATCH["ps"] = ("psum", [128, 4096], "float32")
 for _t in range(NR + 1):
     SCRATCH["xt%d" % _t] = ("sbuf", [128, 4 * C], "bfloat16")
     SCRATCH["qx%d" % _t] = ("sbuf", [128, E], "float8_e4m3fn_x4")
@@ -53,7 +32,7 @@ DMAS = ["dxa", "dxb", "du", "dv", "dwc", "dws", "dlv", "dya", "dyb", "dca", "dcb
 SEMAPHORES = ["vec", "act", "ten", "pool", "left"] + ["arr%d" % t for t in range(NR)] + DMAS
 
 ADD, SUB, MUL, MAX = AluOpType.add, AluOpType.subtract, AluOpType.mult, AluOpType.max
-GT, LT, LE, EQ = AluOpType.is_gt, AluOpType.is_lt, AluOpType.is_le, AluOpType.is_equal
+GT, LT, GE, EQ = AluOpType.is_gt, AluOpType.is_lt, AluOpType.is_ge, AluOpType.is_equal
 COPY, IDEN, SIGN = ActivationFunctionType.Copy, ActivationFunctionType.Identity, ActivationFunctionType.Sign
 CENTER = 5380840.0
 
@@ -130,10 +109,10 @@ def rank_program(g, core, T, topo):
     def quant(codes, plane, src, lo, hi, R):
         op("v", R, [(codes, lo, hi)], g.vector.quantize_mx, V(codes, lo, hi), V(plane, lo, hi), V(src, 4 * lo, 4 * hi))
 
-    def mx(bank, cols, l, ls, llo, r, rs, rlo, rhi):
-        op("t", [(l, llo, llo + 128), (r, rlo, rhi)], [("b%d" % bank, 0, 1)], g.tensor.matmul_mx,
+    def mx(bank, cols, l, ls, llo, r, rs, rlo, rhi, start=True, stop=True):
+        op("t", [(l, llo, llo + 128), (r, rlo, rhi)], [("b%d" % bank, 0, 512)], g.tensor.matmul_mx,
            T.ps[:, 512 * bank:512 * bank + cols], V(l, llo, llo + 128), V(ls, llo, llo + 128),
-           V(r, rlo, rhi), V(rs, rlo, rhi), True, True)
+           V(r, rlo, rhi), V(rs, rlo, rhi), start, stop)
 
     def bank(k, lo, hi):
         return T.ps[:, 512 * k + lo:512 * k + hi]
@@ -160,150 +139,190 @@ def rank_program(g, core, T, topo):
     fill("hb", 0, 128, 0.5)
     op("g", [], [("uo", 0, 16)], g.iota, T.uo[:, :], [[1, 2], [16, 8]], 0, 0)
     op("g", [], [("pin", 0, 1)], g.iota, T.pin[:, :], [[0, 1]], 0, 1)
+    op("g", [], [("qi", 0, 16)], g.iota, T.qi[:, :], [[1, 16]], 0, 0, allow_small_or_imprecise_dtypes=True)
     op("g", [("hb", 0, 128)], [("ident", 0, 128)], g.affine_select, T.ident[:, :], T.hb[:, :], [[-1, 128]], EQ, 0.0, 0, 1)
-    op("g", [], [("iof", 0, E)], g.iota, T.iof[:, :], [[1, E]], 0, 0, allow_small_or_imprecise_dtypes=True)
-    fill("et", 0, 2048, 0.0)
-    tc(T.uo16[:, :], T.uo[:, :], [("uo", 0, 16)], [("uo16", 0, 16)])
-    op("v", [("pin", 0, 1)], [("pod", 0, 1)], g.vector.tensor_scalar, T.pod[:, :], T.pin[:, :], 4, 1, AluOpType.logical_shift_right, AluOpType.bitwise_and)
-    op("v", [("pin", 0, 1)], [("pla", 0, 1)], g.vector.tensor_scalar, T.pla[:, :], T.pin[:, :], 15, None, AluOpType.bitwise_and)
-    tc(T.od[:, :], T.pod[:, :], [("pod", 0, 1)], [("od", 0, 1)])
-    tc(T.pl[:, :], T.pla[:, :], [("pla", 0, 1)], [("pl", 0, 1)])
-    ts(T.ev[:, :], T.od[:, :], -1.0, 1.0, MUL, ADD, [("od", 0, 1)], [("ev", 0, 1)])
+    fill("ones", 0, 512, 1.0)
     fill("w5", E, E + 16, -512.0)
     fill("er", E, E + 16, -256.0)
-    fill("lr", E, E + 16, -256.0)
-    fill("ar1", E, E + 16, 0.0)
-    fill("ar2", E, E + 16, 0.0)
-    for nm in ("kr", "ordr"):
-        fill(nm, 0, OFF, 0.0)
-        fill(nm, OFF + E, E + 32, 0.0)
-    fill("ones", 0, E, 1.0)
-    fill("eq", 0, 28, 0.0)
-    fill("ks", 0, 8, -9.0e6)
+    for lo, hi in ((0, OFF), (OFF + E, E + 32)):
+        fill("ordr", lo, hi, 0.0)
+    tc(T.uo16[:, :], T.uo[:, :], [("uo", 0, 16)], [("uo16", 0, 16)])
+    for nm, a, b in (("pla", 15, None), ("plq", 2, 3), ("pod", 4, 1)):
+        if b is None:
+            op("v", [("pin", 0, 1)], [(nm, 0, 1)], g.vector.tensor_scalar, T[nm][:, :], T.pin[:, :], a, b, AluOpType.bitwise_and)
+        else:
+            op("v", [("pin", 0, 1)], [(nm, 0, 1)], g.vector.tensor_scalar, T[nm][:, :], T.pin[:, :], a, b, AluOpType.logical_shift_right, AluOpType.bitwise_and)
+    for nm, src in (("pl", "pla"), ("pq", "plq"), ("od", "pod")):
+        tc(T[nm][:, :], T[src][:, :], [(src, 0, 1)], [(nm, 0, 1)])
+    ts(T.ev[:, :], T.od[:, :], -1.0, 1.0, MUL, ADD, [("od", 0, 1)], [("ev", 0, 1)])
+    ts(T.lama[:, :], T.pq[:, :], 512.0, 512.0, MUL, ADD, [("pq", 0, 1)], [("lama", 0, 1)])
+    ts(T.lam[:, :], T.pl[:, :], 512.0, T.lama[:, 0:1], MUL, ADD, [("pl", 0, 1), ("lama", 0, 1)], [("lam", 0, 1)])
+    for nm, c in (("lamb", -512.0), ("lams", -256.0)):
+        ts(T[nm][:, :], T.lam[:, :], c, None, ADD, None, [("lam", 0, 1)], [(nm, 0, 1)])
+    fill("et", 0, 2048, 0.0)
     for b in range(4):
         tc(T.et[:, 512 * b + b:512 * b + 512:4], T.ident[:, :], [("ident", 0, 128)], [("et", 512 * b, 512 * b + 512)])
     quant("qx0", "sx0", "xt0", 0, 128, xr(0, 0, 128))
     send(0)
+    op("g", [("ones", 0, 512)], [("ga", 0, 512)], g.affine_select, T.ga[:, :], T.ones[:, :], [[-16, 8], [0, 64]], GE, 0.0, 0, 1)
+    op("g", [("ga", 0, 512)], [("gt", 0, 512)], g.affine_select, T.gt[:, :], T.ga[:, :], [[16, 8], [0, 64]], GE, 0.0, 15, -1)
+    op("g", [], [("iom", 0, E)], g.iota, T.iom[:, :], [[1, E]], -192, 0, allow_small_or_imprecise_dtypes=True)
+    op("g", [], [("iof", 0, E)], g.iota, T.iof[:, :], [[1, E]], 0, 0, allow_small_or_imprecise_dtypes=True)
     quant("qu", "su", "ut", 0, 128, [("ut", 0, 128)])
     op("v", [("qu", 0, 128), ("uo16", 0, 16)], [("qur", 0, 256)], g.vector.tensor_copy,
        T.qur[:, 0:256].bitcast(dt.uint32), T.qu[:, 0:128].bitcast(dt.uint32).indirect(T.uo16[:, 0:16]))
+    act(V("hl", 2, 1920, 4), V("ones", 0, 480), COPY, [("ones", 0, 512)], [("hl", 2, 3)], scale=0.0)
+    act(V("hl", 3, 1920, 4), V("ones", 0, 480), COPY, [("ones", 0, 512)], [("hl", 3, 4)], scale=0.0)
     op("a", [("qu", 0, 128), ("uo16", 0, 16)], [("qurs", 0, 256)], g.scalar.activation,
        T.sur[:, 0:256], T.su[:, 0:128].indirect(T.uo16[:, 0:16]), COPY)
+    for b in range(2):
+        act(V("hl", b, 64, 4), V("ones", 0, 16), COPY, [("ones", 0, 512)], [("hl", 4 + b, 5 + b)], scale=0.0)
+        act(V("hl", 4 * (OFF + E) + b, 1920, 4), V("ones", 0, 16), COPY, [("ones", 0, 512)], [("hl", 6 + b, 7 + b)], scale=0.0)
     quant("qx0", "sx0", "xt0", 128, C, xr(0, 128, C))
     quant("qe", "se", "et", 0, 512, [("et", 0, 2048)])
-    ts(T.iom[:, :], T.iof[:, :], -192.0, None, ADD, None, [("iof", 0, E)], [("iom", 0, E)])
-    quant("qv", "sv", "vt", 0, 128, [("vt", 0, 128)])
-    op("g", [], [("qrow", 0, E)], g.iota, T.qrow[:, :], [[0, 28], [1, 16]], 0, 0, allow_small_or_imprecise_dtypes=True)
     for b in range(4):
         act(V("vp", E * b, E * b + C), V("xt0", b, 4 * C, 4), COPY, [("x0_%d" % b, 0, C)], [("vp%d" % b, 0, C)], scale=0.5)
     waits("t", [("qurs", 0, 256)], [])
 
-    def wrap(src, ta, tb, a1, a2, out, dtype_tag):
-        op("v", [(src, OFF, OFF + E)], [(ta, 0, E)], g.vector.transpose, V(ta, 0, E), V(src, OFF, OFF + E))
-        op("v", [(src, 0, E + 32)], [(tb, 0, E)], g.vector.transpose, V(tb, 0, E + 32), V(src, 0, E + 32))
-        A, B = [(ta, 0, E)], [(tb, 0, E)]
-        ts(V(a1, 0, 28, 2), V(ta, 0, E, 32), T.ev[:, 0:1], None, MUL, None, A + [("ev", 0, 1)], [(a1 + "e", 0, 1)])
-        ts(V(a2, 1, 28, 2), V(ta, 16, E, 32), T.od[:, 0:1], None, MUL, None, A + [("od", 0, 1)], [(a2 + "o", 0, 1)])
-        ts(V(a2, 0, 28, 2), V(tb, 16, E, 32), T.od[:, 0:1], None, MUL, None, B, [(a2 + "e", 0, 1)])
-        ts(V(a1, 1, 28, 2), V(tb, 32, E + 32, 32), T.ev[:, 0:1], None, MUL, None, B, [(a1 + "o", 0, 1)])
-        tt(V(out, 0, 28), V(a1, 0, 28), V(a2, 0, 28), ADD,
-           [(a1 + "e", 0, 1), (a2 + "o", 0, 1), (a2 + "e", 0, 1), (a1 + "o", 0, 1)], [(out, 0, 28)])
+    def wrap(row, reg, ta, tb, out):
+        op("v", reg, [(ta, 0, E)], g.vector.transpose, V(ta, 0, E), row(OFF, OFF + E))
+        op("v", reg, [(tb, 0, E)], g.vector.transpose, V(tb, 0, E + 32), row(0, E + 32))
+        tt(V("o1", 0, 28), V(ta, 0, E, 16), V("ma", 0, 28), MUL, [(ta, 0, E), ("ma", 0, 2)], [("o1", 0, 28)])
+        tt(V("o2", 0, 28), V(tb, 16, E + 16, 16), V("mb", 0, 28), MUL, [(tb, 0, E), ("mb", 0, 2)], [("o2", 0, 28)])
+        tt(V(out, 0, 28), V("o1", 0, 28), V("o2", 0, 28), ADD, [("o1", 0, 28), ("o2", 0, 28)], [(out, 0, 28)])
+
+    def words0(k, sl, sh, lo, hi, klo, khi):
+        ts(V("t1", lo, hi), bank(k, sl, sh), 0.0, 1024.0, GT, MUL, [("b%d" % k, 0, 1)], [("t1", lo, hi)])
+        ts(V("t2", lo, hi), bank(k + 1, sl, sh), 0.0, 512.0, GT, MUL, [("b%d" % (k + 1), 0, 1)], [("t2", lo, hi)])
+        tt(V("w5", lo, hi), V("t1", lo, hi), V("t2", lo, hi), ADD, [("t1", lo, hi), ("t2", lo, hi)], [("w5", lo, hi)])
+        ts(V("w6", klo, khi), V("w5", klo, khi), 5.0, 512.0, MUL, ADD, [("w5", klo, khi)], [("w6", klo, khi)])
+        tt(V("er", klo, khi), V("w6", klo, khi), V("w5", klo + 1, khi + 1), ADD, [("w6", klo, khi), ("w5", klo + 1, khi + 1)], [("er", klo, khi)])
+
+    def words(t, k, sl, sh, lo, hi):
+        d = 2 ** t
+        ar, klo, khi = "ar%d" % t, max(lo - d, 0), hi if hi == E else hi - d
+        unit, fac = ((512.0, 41.0), (1.0, 3281.0))[t - 1]
+        ts(V(ar, lo, hi), bank(k, sl, sh), 0.0, unit, GT, MUL, [("b%d" % k, 0, 1)], [(ar, lo, hi)])
+        ts(V("al", klo, khi), V(ar, klo, khi), fac, None, MUL, None, [(ar, klo, khi)], [("al", klo, khi)])
+        tt(V("ag", klo, khi), V("al", klo, khi), V("g1", klo, khi), ADD, [("al", klo, khi), ("g1", klo, khi)], [("ag", klo, khi)])
+        tt(V("kr", OFF + klo, OFF + khi), V("ag", klo, khi), V(ar, klo + d, khi + d), ADD,
+           [("ag", klo, khi), (ar, klo + d, khi + d)], [("kr", OFF + klo, OFF + khi)])
+        if t == NR - 1:
+            for o, e in ((0, 0.5), (E, -0.5)):
+                act(V("d2", o + klo, o + khi), V("kr", OFF + klo, OFF + khi), IDEN, [("kr", OFF + klo, OFF + khi)], [("d2", o + klo, o + khi)], bias=e)
+
+    K = V("kr", OFF, OFF + E)
+    KR = [("kr", OFF, OFF + E)]
 
     for t in range(NR):
-        d = 2 ** t
         qx, sx = "qx%d" % t, "sx%d" % t
-        mx(0, E, "qur", "sur", 0, qx, sx, 0, E)
+        last = t == NR - 1
         if t == 0:
-            mx(1, E, "qur", "sur", 128, qx, sx, 0, E)
+            mx(0, C, "qur", "sur", 0, qx, sx, 0, C)
+            mx(1, C, "qur", "sur", 128, qx, sx, 0, C)
+            words0(0, 0, C, 0, C, 0, C - 1)
+            for nm, a, b in (("ma", "ev", "od"), ("mb", "od", "ev")):
+                ts(V(nm, 0, 28, 2), V("ones", 0, 14), T[a][:, 0:1], None, MUL, None, [("ones", 0, 512), (a, 0, 1)], [(nm, 0, 1)])
+                ts(V(nm, 1, 28, 2), V("ones", 0, 14), T[b][:, 0:1], None, MUL, None, [("ones", 0, 512), (b, 0, 1)], [(nm, 1, 2)])
+            mx(2, 128, "qur", "sur", 0, qx, sx, E - 128, E)
+            mx(3, 128, "qur", "sur", 128, qx, sx, E - 128, E)
+        else:
+            mx(1, E - 128, "qur", "sur", 0, qx, sx, 128, E)
         for b in range(4):
             mx(4 + b, 128, "qe", "se", 128 * b, qx, sx, E - 128, E)
-        K = V("kr", OFF, OFF + E)
-        KR = [("kr", OFF, OFF + E)]
         if t == 0:
-            ts(V("t1", 0, E), bank(0, 0, E), 0.0, 1024.0, GT, MUL, [("b0", 0, 1)], [("t1", 0, E)])
-            ts(V("t2", 0, E), bank(1, 0, E), 0.0, 512.0, GT, MUL, [("b1", 0, 1)], [("t2", 0, E)])
-            tt(V("w5", 0, E), V("t1", 0, E), V("t2", 0, E), ADD, [("t1", 0, E), ("t2", 0, E)], [("w5", 0, E)])
-            ts(V("w6", 0, E), V("w5", 0, E), 5.0, 512.0, MUL, ADD, [("w5", 0, E)], [("w6", 0, E)])
-            tt(V("er", 0, E), V("w6", 0, E), V("w5", 1, E + 1), ADD, [("w6", 0, E), ("w5", 0, E + 16)], [("er", 0, E)])
-            tt(K, V("er", 0, E), V("iof", 0, E), ADD, [("er", 0, E), ("iof", 0, E)], KR)
+            words0(2, 64, 128, C, E, C - 1, E)
+            act(V("junk", 0, E), V("er", 0, E), SIGN, [("er", 0, E), ("lams", 0, 1)], [("junk0", 0, 1), ("acc", 0, 1)],
+                bias=T.lams[:, 0:1], scale=-1.0, accum_out=T.acc[:, 0:1])
         else:
-            ar = "ar%d" % t
-            unit, fac = ((512.0, 41.0), (1.0, 3281.0))[t - 1]
-            ts(V(ar, 0, E), bank(0, 0, E), 0.0, unit, GT, MUL, [("b0", 0, 1)], [(ar, 0, E)])
-            ts(V("al", 0, E), V(ar, 0, E), fac, None, MUL, None, [(ar, 0, E)], [("al", 0, E)])
-            tt(V("ag", 0, E), V("al", 0, E), V("g1", 0, E), ADD, [("al", 0, E), ("g1", 0, E)], [("ag", 0, E)])
-            tt(K, V("ag", 0, E), V(ar, d, E + d), ADD, [("ag", 0, E), (ar, 0, E + 16)], KR)
+            words(t, 1, 0, E - 128, 128, E)
         for b in range(4):
             act(V("vp", E * b + C, E * b + E), bank(4 + b, 64, 128), COPY, [("b%d" % (4 + b), 0, 1)], [("vp%d" % b, C, E)])
-        last = t == NR - 1
-        if last:
-            act(V("dd", E, 2 * E), K, IDEN, KR, [("dd", E, 2 * E)], bias=-0.5)
-            act(V("dd", 0, E), K, IDEN, KR, [("dd", 0, E)], bias=0.5)
-        wrap("kr", "ka", "kb", "o1", "o2", "own", "f")
         ns = NS[t]
         nv = 28 - ns
-        half = nv // 2
-
-        def row(c):
-            if last:
-                return V("dd", 16 * c + 16, 16 * c + 16 + E), [("dd", 16 * c + 16, 16 * c + 16 + E)]
-            return K, KR
-
-        for c in range(ns):
-            v, r = row(c)
-            j = c % 4
-            act(V("junk", E * j, E * j + E), v, SIGN, r + [("own", 0, 28)], [("junk%d" % j, 0, 1), ("acc", c, c + 1)],
-                bias=T.own[:, c:c + 1], scale=-1.0, accum_out=T.acc[:, c:c + 1])
-        for k in range(nv):
-            v, r = row(ns + k)
-            o = [("cb", k, k + 1)]
-            if k < half:
-                ts(V("cb", E * k, E * k + E), v, T.own[:, ns + k:ns + k + 1], None, LT, None, r + [("own", 0, 28)], o)
-            else:
-                ts(V("cb", E * k, E * k + E), v, T.own[:, ns + k:ns + k + 1], 1024.0, LT, MUL, r + [("own", 0, 28)], o)
-        for k in range(half):
-            op("v", [("cb", k, k + 1), ("cb", half + k, half + k + 1)], [("sc", k, k + 1)], g.vector.tensor_tensor_scan,
-               V("sc", E * k, E * k + E), V("cb", E * k, E * k + E), V("cb", E * (half + k), E * (half + k) + E), 0.0, ADD, ADD)
-        if last:
-            tt(V("kt", 0, E), K, V("tri", 0, E), ADD, KR + [("tri", 0, E)], [("kt", 0, E)])
-            for q in range(1, 16):
-                tt(V("eq", 28 * q, 28 * q + 28), V("kt", q, E, 16), V("own", 0, 28), EQ, [("kt", 0, E), ("own", 0, 28)], [("eq", 28 * q, 28 * q + 28)])
-            tt(V("f1", 0, 224), V("eq", 0, 224), V("eq", 224, 448), ADD, [("eq", 0, 448)], [("f1", 0, 1)])
-            tt(V("f2", 0, 112), V("f1", 0, 112), V("f1", 112, 224), ADD, [("f1", 0, 1)], [("f2", 0, 1)])
-            tt(V("f3", 0, 56), V("f2", 0, 56), V("f2", 56, 112), ADD, [("f2", 0, 1)], [("f3", 0, 1)])
-            tt(V("f4", 0, 28), V("f3", 0, 28), V("f3", 28, 56), ADD, [("f3", 0, 1)], [("f4", 0, 1)])
-        tc(V("i1", 0, half), V("sc", E - 1, E * half, E), [("sc", 0, half)], [("i1", 0, 1)])
-        op("v", [("i1", 0, 1)], [("i2", 0, 1)], g.vector.tensor_scalar, V("i2", 0, half), V("i1", 0, half), 1023, None, AluOpType.bitwise_and)
-        op("v", [("i1", 0, 1)], [("i2", 1, 2)], g.vector.tensor_scalar, V("i2", half, nv), V("i1", 0, half), 10, None, AluOpType.logical_shift_right)
-        if not last:
-            tc(V("pos", ns, 28), V("i2", 0, nv), [("i2", 0, 2)], [("pos", ns, 28)])
-            ts(V("pos", 0, ns), V("acc", 0, ns), 0.5, 223.5, MUL, ADD, [("acc", 0, ns)], [("pos", 0, ns)])
+        if t == 0:
+            act(V("s1", 0, E), V("er", 0, E), IDEN, [("er", 0, E)], [("s1", 0, E)], bias=512.0, scale=82.0)
+            act(V("s2", 0, E), V("er", 2, E + 2), COPY, [("er", 0, E + 16)], [("s2", 0, E)], scale=2.0)
+            for b in range(4):
+                act(V("x32", C * b, C * b + C), V("xt0", b, 4 * C, 4), COPY, [("x0_%d" % b, 0, C)], [("x32_%d" % b, 0, C)], scale=32.0)
+            O = V("cb", 0, E)
+            ts(V("cb", 0, E - 1), V("er", 0, E - 1), T.lam[:, 0:1], None, EQ, None, [("er", 0, E), ("lam", 0, 1)], [("cb", 0, 1)])
+            ts(V("cb", E - 1, E), V("er", E - 1, E), T.lamb[:, 0:1], None, EQ, None, [("er", 0, E), ("lamb", 0, 1)], [("cb", 1, 2)])
+            quant("qg", "sg", "gt", 0, 128, [("gt", 0, 512)])
+            ts(T.first[:, :], T.acc[:, 0:1], 0.5, 31.0, MUL, ADD, [("acc", 0, 1)], [("first", 0, 1)])
+            op("v", [("cb", 0, 2), ("ones", 0, 512), ("first", 0, 1)], [("t1", 0, E)], g.vector.tensor_tensor_scan,
+               V("t1", 0, E), V("ones", 0, E), O, T.first[:, 0:1], MUL, ADD)
+            tc(V("t1", E - 1, E), T.first[:, 0:1], [("first", 0, 1)], [("t1", E - 1, E)])
+            tt(V("t2", 0, E), V("t1", 0, E), O, MUL, [("t1", 0, E), ("cb", 0, 2)], [("t2", 0, E)])
+            ts(V("w6", 0, E), V("t2", 0, E), 3072.0, None, ADD, None, [("t2", 0, E)], [("w6", 0, E)])
+            d0, d1 = V("hl", 4 * OFF, 4 * (OFF + E), 4), V("hl", 4 * OFF + 1, 4 * (OFF + E), 4)
+            ts(d0, V("w6", 0, E), -3072.0, None, ADD, None, [("w6", 0, E)], [("hl", 0, 1)])
+            tt(d1, V("t2", 0, E), d0, SUB, [("t2", 0, E), ("hl", 0, 1)], [("hl", 1, 2)])
+            quant("qh", "sh", "hl", 0, E + 32, [("hl", 0, 8)])
+            mx(3, E + 32, "qg", "sg", 0, "qh", "sh", 0, E + 32)
+            tt(V("g1", 0, E), V("s1", 0, E), V("iof", 0, E), ADD, [("s1", 0, E), ("iof", 0, E)], [("g1", 0, E)])
+            wrap(lambda lo, hi: bank(3, lo, hi), [("b3", 0, 1)], "ka", "kb", "p3")
+            ts(V("pos", 0, 28), V("p3", 0, 28), 192.0, None, ADD, None, [("p3", 0, 28)], [("pos", 0, 28)])
         else:
-            ts(V("posf", ns, 28), V("i2", 0, nv), -1.0, None, ADD, None, [("i2", 0, 2)], [("posf", ns, 28)])
-            ts(V("posf", 0, ns), V("acc", 0, ns), 0.5, 223.0, MUL, ADD, [("acc", 0, ns)], [("posf", 0, ns)])
-            tt(V("f4", 0, 28), V("posf", 0, 28), V("f4", 0, 28), SUB, [("posf", 0, 28), ("f4", 0, 1)], [("f4", 0, 1)])
-            tc(V("pos", 0, 28), V("f4", 0, 28), [("f4", 0, 1)], [("pos", 0, 28)])
+            wrap(lambda lo, hi: V("kr", lo, hi), [("kr", 0, E + 32)], "ka", "kb", "own")
+
+            def row(c):
+                if not last:
+                    return K, KR
+                return V("d2", 16 * c + 16, 16 * c + 16 + E), [("d2", 16 * c + 16, 16 * c + 16 + E)]
+
+            for c in range(ns):
+                v, r = row(c)
+                j = c % 4
+                act(V("junk", E * j, E * j + E), v, SIGN, r + [("own", 0, 28)], [("junk%d" % j, 0, 1), ("acc", c, c + 1)],
+                    bias=T.own[:, c:c + 1], scale=-1.0, accum_out=T.acc[:, c:c + 1])
+            if last:
+                for q in range(1, 16):
+                    o = 112 * (q // 4) + q % 4
+                    tt(V("eq", o, 112 * (q // 4) + 112, 4), V("kr", OFF + q, OFF + E, 16), V("own", 0, 28), EQ, KR + [("own", 0, 28)], [("eq", 1000 + q, 1001 + q)])
+                quant("qq", "sq", "eq", 0, 212, [("eq", 0, 1016)])
+                for k in range(4):
+                    mx(3, 128, "qc", "cs", 128 * k, "qq", "sq", 28 * k, 28 * k + 128, k == 0, k == 3)
+            for k in range(nv):
+                v, r = row(ns + k)
+                ts(V("cb", E * k, E * k + E), v, T.own[:, ns + k:ns + k + 1], None, LT, None, r + [("own", 0, 28)], [("cb", k, k + 1)])
+            for k in range(nv):
+                op("v", [("cb", k, k + 1)], [("sc", k, k + 1)], g.vector.tensor_tensor_scan, V("sc", 224 * k, 224 * k + 224),
+                   V("cb", E * k, E * k + 224), V("cb", E * k + 224, E * k + E), -192.0, ADD, ADD)
+            cnt = V("sc", 223, 224 * nv, 224)
+            if not last:
+                ts(V("pos", ns, 28), cnt, 192.0, None, ADD, None, [("sc", 0, nv)], [("pos", ns, 28)])
+                ts(V("pos", 0, ns), V("acc", 0, ns), 0.5, 223.5, MUL, ADD, [("acc", 0, ns)], [("pos", 0, ns)])
+            else:
+                ts(V("posf", ns, 28), cnt, 191.0, None, ADD, None, [("sc", 0, nv)], [("posf", ns, 28)])
+                ts(V("posf", 0, ns), V("acc", 0, ns), 0.5, 223.0, MUL, ADD, [("acc", 0, ns)], [("posf", 0, ns)])
+                tt(V("posg", 0, 28), V("posf", 0, 28), bank(3, 0, 28), SUB, [("posf", 0, 28), ("b3", 0, 1)], [("posg", 0, 28)])
+                tc(V("pos", 0, 28), V("posg", 0, 28), [("posg", 0, 28)], [("pos", 0, 28)])
         tc(V("ordr", OFF, OFF + E).indirect(V("pos", 0, 28)), V("iom", 0, E), [("iom", 0, E), ("pos", 0, 28)], [("ordr", OFF, OFF + E)])
-        wrap("ordr", "oa", "ob", "p1", "p2", "p3", "b")
+        wrap(lambda lo, hi: V("ordr", lo, hi), [("ordr", 0, E + 32)], "oa", "ob", "p3")
         ts(V("ordl", 0, 28), V("p3", 0, 28), 192.0, None, ADD, None, [("p3", 0, 28)], [("ordl", 0, 28)])
         for b in range(4):
             act(V("vs", E * b, E * b + E), V("vp", E * b, E * b + E).indirect(V("ordl", 0, 28)), COPY,
                 [("vp%d" % b, 0, E), ("ordl", 0, 28)], [("vs%d" % b, 0, 1)])
         if last:
-            act(V("ks", 1, 1 + E), V("kr", OFF, OFF + E).indirect(V("ordl", 0, 28)), COPY, KR + [("ordl", 0, 28)], [("ks", 1, 1 + E)])
+            act(V("ks", 1, 1 + E), K.indirect(V("ordl", 0, 28)), COPY, KR + [("ordl", 0, 28)], [("ks", 1, 1 + E)])
         if t == 0:
-            for b in range(4):
-                act(V("x32", C * b, C * b + C), V("xt0", b, 4 * C, 4), COPY, [("x0_%d" % b, 0, C)], [("x32_%d" % b, 0, C)], scale=32.0)
-            act(V("s1", 0, E), V("er", 0, E), IDEN, [("er", 0, E)], [("s1", 0, E)], bias=512.0, scale=82.0)
-            act(V("s2", 0, E), V("er", 2, E + 2), COPY, [("er", 0, E + 16)], [("s2", 0, E)], scale=2.0)
+            tt(V("g1", 0, E), V("g1", 0, E), V("s2", 0, E), ADD, [("g1", 0, E), ("s2", 0, E)], [("g1", 0, E)])
+        elif t == 1:
+            fill("lr", E, E + 16, -256.0)
+            tt(V("lr", 0, E), K, V("iof", 0, E), SUB, KR + [("iof", 0, E)], [("lr", 0, E)])
+            act(V("s1", 0, E), V("lr", 0, E), IDEN, [("lr", 0, E)], [("s1", 0, E)], bias=1.0 - CENTER, scale=6562.0 / 512.0)
+            act(V("s2", 0, E), V("lr", 4, E + 4), COPY, [("lr", 0, E + 16)], [("s2", 0, E)], scale=1.0 / 256.0)
         for b in range(4):
             o = E * b
             tt(V("mm", o + 1, o + E - 1), V("vs", o, o + E - 2), V("vs", o + 2, o + E), MAX, [("vs%d" % b, 0, 1)], [("mm%d" % b, 0, 1)])
-            tt(V("mm", o, o + E, E - 1), V("vs", o, o + E, E - 1), V("vs", o + 1, o + E - 1, E - 3), MAX, [("vs%d" % b, 0, 1)], [("mm%d" % b, 1, 2)])
+        ends = [("vs%d" % b, 0, 1) for b in range(4)]
+        tt(V("mm", 0, 4 * E, E), V("vs", 0, 4 * E, E), V("vs", 1, 4 * E, E), MAX, ends, [("mm%d" % b, 1, 2) for b in range(4)])
+        tt(V("mm", E - 1, 4 * E, E), V("vs", E - 1, 4 * E, E), V("vs", E - 2, 4 * E, E), MAX, ends, [("mm%d" % b, 2, 3) for b in range(4)])
 
         def fused(b, lo, hi):
             tt(V("zt", 4 * lo + b, 4 * hi, 4), V("mm", E * b, E * b + E).indirect(V("pos", lo // 16, hi // 16)), V("vp", E * b + lo, E * b + hi), ADD,
-               [("mm%d" % b, 0, 2), ("pos", 0, 28), ("vp%d" % b, lo, hi)], [("z%d" % b, lo, hi)])
+               [("mm%d" % b, 0, 3), ("pos", 0, 28), ("vp%d" % b, lo, hi)], [("z%d" % b, lo, hi)])
 
         def product(lo, hi, b0):
             quant("qz", "sz", "zt", lo, hi, [("z%d" % b, lo, hi) for b in range(4)])
@@ -337,44 +356,55 @@ def rank_program(g, core, T, topo):
         quant(qn, sn, xn, 0, 128, xr(t + 1, 0, 128))
         if not last:
             send(t + 1)
+            mx(0, 128, "qur", "sur", 0, qn, sn, 0, 128)
             planes(0, 128)
         else:
             dma("s", "dca", [(qn, 0, 128)], [], T.oc[:, 0:512], V(qn, 0, 128).bitcast(dt.uint8))
+            mx(0, 128, "qv", "sv", 0, qn, sn, 0, 128)
+            act(V("yr", 0, 128), bank(0, 0, 128), COPY, [("b0", 0, 1)], [("yr", 0, 128)])
+            dma("s", "dya", [("yr", 0, 128)], [], T.y[:, 0:128], T.yr[:, 0:128])
         fused(2, 128, C)
         fused(3, 128, C)
         product(128, C, 4)
         if t == 0:
-            tt(V("g1", 0, E), V("s1", 0, E), V("s2", 0, E), ADD, [("s1", 0, E), ("s2", 0, E)], [("g1", 0, E)])
-            tt(V("g1", 0, E), V("g1", 0, E), V("iof", 0, E), ADD, [("g1", 0, E), ("iof", 0, E)], [("g1", 0, E)])
+            fill("ar1", E, E + 16, 0.0)
+            fill("ar2", E, E + 16, 0.0)
+            for lo, hi in ((0, OFF), (OFF + E, E + 32)):
+                fill("kr", lo, hi, 0.0)
+            fill("eq", 0, 848, 0.0)
+            ts(T.behind[:, :], T.qi[:, :], T.pl[:, 0:1], 2.0, GT, MUL, [("qi", 0, 16), ("pl", 0, 1)], [("behind", 0, 16)])
         elif t == 1:
-            tt(V("lr", 0, E), K, V("iof", 0, E), SUB, KR + [("iof", 0, E)], [("lr", 0, E)])
-            act(V("s1", 0, E), V("lr", 0, E), IDEN, [("lr", 0, E)], [("s1", 0, E)], bias=1.0 - CENTER, scale=6562.0 / 512.0)
-            act(V("s2", 0, E), V("lr", 4, E + 4), COPY, [("lr", 0, E + 16)], [("s2", 0, E)], scale=1.0 / 256.0)
+            tt(V("g1", 0, E), V("s1", 0, E), V("s2", 0, E), ADD, [("s1", 0, E), ("s2", 0, E)], [("g1", 0, E)])
         else:
             tt(V("eqs", 0, E), V("ks", 1, E + 1), V("ks", 0, E), EQ, [("ks", 0, E + 1)], [("eqs", 0, E)])
-            op("v", [("ones", 0, E), ("eqs", 0, E)], [("rr", 0, E)], g.vector.tensor_tensor_scan, V("rr", 0, E), V("ones", 0, E), V("eqs", 0, E), 0.0, ADD, MUL)
-            tt(V("lw", 0, E), V("iof", 0, E), V("rr", 0, E), SUB, [("iof", 0, E), ("rr", 0, E)], [("lw", 0, E)])
+            op("v", [("ones", 0, 512), ("eqs", 0, E)], [("rr", 0, E)], g.vector.tensor_tensor_scan, V("rr", 0, E), V("ones", 0, E), V("eqs", 0, E), 0.0, ADD, MUL)
         update(128, C, 4)
         quant(qn, sn, xn, 128, C, xr(t + 1, 128, C))
-        if t == 0:
-            ts(V("tri", 0, E), V("qrow", 0, E), T.pl[:, 0:1], 16777216.0, LE, MUL, [("qrow", 0, E), ("pl", 0, 1)], [("tri", 0, E)])
         if t == 1:
-            tt(V("g1", 0, E), V("s1", 0, E), V("s2", 0, E), ADD, [("s1", 0, E), ("s2", 0, E)], [("g1", 0, E)])
+            quant("qc", "cs", "ct", 0, 512, [("ct", 0, 16)])
+            quant("qv", "sv", "vt", 0, 128, [("vt", 0, 128)])
+            fill("ks", 0, 8, -9.0e6)
         if not last:
+            words(t + 1, 0, 0, 128, 0, 128)
             planes(128, C)
+            if t == 0:
+                for q in range(16):
+                    o = 512 * (q // 4)
+                    act(T.ct[:, o + q % 4:o + 512:4], T.ident[:, :], COPY, [("ident", 0, 128), ("behind", 0, 16)], [("ct", q, q + 1)], scale=T.behind[:, q:q + 1])
+        else:
+            tt(V("lw", 0, E), V("iof", 0, E), V("rr", 0, E), SUB, [("iof", 0, E), ("rr", 0, E)], [("lw", 0, E)])
 
     q, s = "qx%d" % NR, "sx%d" % NR
-    mx(0, C, "qv", "sv", 0, q, s, 0, C)
+    mx(1, C - 128, "qv", "sv", 0, q, s, 128, C)
     dma("s", "dcb", [(q, 128, C)], [], T.oc[:, 512:1536], V(q, 128, C).bitcast(dt.uint8))
-    act(V("lvr", 0, E), V("lw", 0, E).indirect(V("pos", 0, 28)), COPY, [("lw", 0, E), ("pos", 0, 28)], [("lvr", 0, E)])
-    tc(T.yr[:, :], bank(0, 0, C), [("b0", 0, 1)], [("yr", 0, C)])
-    dma("a", "dya", [("yr", 0, C)], [], T.y[:, :], T.yr[:, :])
     for k in range(4):
         dma("s", "ds%d" % k, [(q, 0, C)], [], T.osc[4 * k:4 * k + 4, 0:C], T[s][32 * k:32 * k + 4, 0:C])
+    act(V("yr", 128, C), bank(1, 0, C - 128), COPY, [("b1", 0, 1)], [("yr", 128, C)])
+    dma("a", "dyb", [("yr", 128, C)], [], T.y[:, 128:C], T.yr[:, 128:C])
+    act(V("lvr", 0, E), V("lw", 0, E).indirect(V("pos", 0, 28)), COPY, [("lw", 0, E), ("pos", 0, 28)], [("lvr", 0, E)])
     dma("s", "dlv", [("lvr", 0, E)], [], T.lv[:, :], T.lvr[0:128:16, 0:E])
     for sem in count:
         g.wait_ge(T.sem[sem], count[sem])
     for sem in DMAS:
-        if sem != "dyb":
-            g.wait_ge(T.sem[sem], 16)
+        g.wait_ge(T.sem[sem], 16)
     g.wait_ge(T.sem.left, 2 * NR * len(send_engines(core, prev)))

@@ -1,25 +1,23 @@
 from concourse.mybir import dt, AluOpType, ActivationFunctionType
 
 C, H, E, NR = 384, 64, 448, 3
-OFF = 16
 NS = (0, 16, 18)
 
 SCRATCH = {}
-for _k, _n in (("qu", 128), ("qur", 256), ("qv", 128), ("qw", 512), ("qe", 512), ("qc", 512), ("qz", C), ("qq", 212), ("qg", 128), ("qh", E + 32)):
+for _k, _n in (("qu", 128), ("qur", 256), ("qv", 128), ("qw", 512), ("qe", 512), ("qz", C), ("qg", 128), ("qh", E)):
     SCRATCH[_k] = ("sbuf", [128, _n], "float8_e4m3fn_x4")
-    SCRATCH[{"qc": "cs"}.get(_k, "s" + _k[1:])] = ("sbuf", [128, _n], "uint8")
-for _k, _n in (("ut", 512), ("vt", 512), ("et", 2048), ("ct", 2048), ("gt", 512), ("ga", 512), ("hl", 4 * (E + 32)), ("zt", 4 * C), ("vp", 4 * E),
-               ("x32", 4 * C), ("vs", 4 * E), ("mm", 4 * E), ("hb", 128), ("ident", 128), ("iom", E), ("ones", 512), ("t1", E), ("t2", E),
-               ("w5", E + 16), ("w6", E), ("er", E + 16), ("ar1", E + 16), ("ar2", E + 16), ("junk", 4 * E), ("cb", 16 * E), ("sc", 8 * E),
-               ("ordr", E + 32), ("oa", E), ("ob", E + 32), ("eq", 848), ("eqs", E)):
+    SCRATCH["s" + _k[1:]] = ("sbuf", [128, _n], "uint8")
+for _k, _n in (("ut", 512), ("vt", 512), ("fv", 516), ("ft", 516), ("gt", 512), ("ga", 512), ("hl", 4 * E), ("zt", 4 * C), ("vp", 4 * E),
+               ("vs", 4 * E), ("mm", 4 * E), ("iom", E), ("im", E), ("dm", E), ("kp", E), ("ones", 512), ("t1", E), ("t2", E),
+               ("w5", E + 16), ("w6", E), ("er", E + 16), ("junk", 4 * E), ("cb", 16 * E), ("sc", 8 * E),
+               ("ordr", E), ("b1", E), ("b2", E), ("eq", E), ("te", E), ("eqs", E), ("sg1", E)):
     SCRATCH[_k] = ("sbuf", [128, _n], "bfloat16")
-for _k, _n in (("iof", E), ("ev", 1), ("od", 1), ("pl", 1), ("pq", 1), ("lama", 1), ("lam", 1), ("lamb", 1), ("lams", 1), ("first", 1),
-               ("qi", 16), ("behind", 16), ("lr", E + 16), ("al", E), ("ag", E), ("g1", E),
-               ("s1", E), ("s2", E), ("kr", E + 32), ("ka", E), ("kb", E + 32), ("ma", 28), ("mb", 28), ("o1", 28), ("o2", 28),
-               ("own", 28), ("acc", 28), ("posf", 28), ("posg", 28), ("p3", 28), ("d2", 2 * E), ("ks", E + 16), ("rr", E), ("lw", E),
-               ("lvr", E), ("yr", C)):
+for _k, _n in (("iof", E), ("ios", E), ("pl", 1), ("pq", 1), ("lama", 1), ("lam", 1), ("lamb", 1), ("lams", 1), ("first", 1),
+               ("ar1", E + 16), ("ar2", E + 16), ("lr", E + 16), ("al", E), ("ag", E), ("ga1", E), ("g1", E), ("s1", E), ("s2", E),
+               ("kr", 2 * E), ("x1", E), ("x2", E), ("own", 28), ("acc", 28), ("ti", 28), ("tj", 28), ("posf", 28),
+               ("ks", E + 16), ("rr", E), ("lw", E), ("lvr", E), ("yr", C)):
     SCRATCH[_k] = ("sbuf", [128, _n], "float32")
-for _k, _n in (("uo", 16), ("pin", 1), ("pod", 1), ("pla", 1), ("plq", 1)):
+for _k, _n in (("uo", 16), ("pin", 1), ("pla", 1), ("plq", 1)):
     SCRATCH[_k] = ("sbuf", [128, _n], "int32")
 for _k, _n in (("uo16", 16), ("pos", 28), ("ordl", 28)):
     SCRATCH[_k] = ("sbuf", [128, _n], "uint16")
@@ -34,7 +32,9 @@ SEMAPHORES = ["vec", "act", "ten", "pool", "left"] + ["arr%d" % t for t in range
 ADD, SUB, MUL, MAX = AluOpType.add, AluOpType.subtract, AluOpType.mult, AluOpType.max
 GT, LT, GE, EQ = AluOpType.is_gt, AluOpType.is_lt, AluOpType.is_ge, AluOpType.is_equal
 COPY, IDEN, SIGN = ActivationFunctionType.Copy, ActivationFunctionType.Identity, ActivationFunctionType.Sign
+TOP = (None, 2048.0, 5381000.5)
 CENTER = 5380840.0
+FAC = (None, 41.0, 3281.0)
 
 
 def rank_program(g, core, T, topo):
@@ -100,6 +100,9 @@ def rank_program(g, core, T, topo):
     def tc(out, in_, R, W):
         op("v", R, W, g.vector.tensor_copy, out, in_)
 
+    def scan(out, a, b, ini, o0, o1, R, W):
+        op("v", R, W, g.vector.tensor_tensor_scan, out, a, b, ini, o0, o1)
+
     def act(out, in_, f, R, W, **kw):
         op("a", R, W, g.scalar.activation, out, in_, f, **kw)
 
@@ -136,60 +139,51 @@ def rank_program(g, core, T, topo):
     dma("s", "dws", [], [("qw", 0, 512)], T.sw[:, :], T.ws[:, :])
     dma("a", "dv", [], [("vt", 0, 128)], T.vt[:, :], T.v[:, :])
     hist["qw"] = [(0, 512, True, "dma", "dwc", 16), (0, 512, True, "dma", "dws", 16)]
-    fill("hb", 0, 128, 0.5)
+    fill("fv", 0, 516, 2.0 ** -6)
     op("g", [], [("uo", 0, 16)], g.iota, T.uo[:, :], [[1, 2], [16, 8]], 0, 0)
     op("g", [], [("pin", 0, 1)], g.iota, T.pin[:, :], [[0, 1]], 0, 1)
-    op("g", [], [("qi", 0, 16)], g.iota, T.qi[:, :], [[1, 16]], 0, 0, allow_small_or_imprecise_dtypes=True)
-    op("g", [("hb", 0, 128)], [("ident", 0, 128)], g.affine_select, T.ident[:, :], T.hb[:, :], [[-1, 128]], EQ, 0.0, 0, 1)
+    op("g", [("fv", 0, 516)], [("ft", 0, 516)], g.affine_select, T.ft[:, :], T.fv[:, :], [[-1, 516]], EQ, 0.0, 3, 4)
+    op("g", [], [("im", 0, E)], g.iota, T.im[:, :], [[0, 28], [1, 16]], 0, 0, allow_small_or_imprecise_dtypes=True)
     fill("ones", 0, 512, 1.0)
     fill("w5", E, E + 16, -512.0)
     fill("er", E, E + 16, -256.0)
-    for lo, hi in ((0, OFF), (OFF + E, E + 32)):
-        fill("ordr", lo, hi, 0.0)
     tc(T.uo16[:, :], T.uo[:, :], [("uo", 0, 16)], [("uo16", 0, 16)])
-    for nm, a, b in (("pla", 15, None), ("plq", 2, 3), ("pod", 4, 1)):
+    for nm, a, b in (("pla", 15, None), ("plq", 2, 3)):
         if b is None:
             op("v", [("pin", 0, 1)], [(nm, 0, 1)], g.vector.tensor_scalar, T[nm][:, :], T.pin[:, :], a, b, AluOpType.bitwise_and)
         else:
             op("v", [("pin", 0, 1)], [(nm, 0, 1)], g.vector.tensor_scalar, T[nm][:, :], T.pin[:, :], a, b, AluOpType.logical_shift_right, AluOpType.bitwise_and)
-    for nm, src in (("pl", "pla"), ("pq", "plq"), ("od", "pod")):
+    for nm, src in (("pl", "pla"), ("pq", "plq")):
         tc(T[nm][:, :], T[src][:, :], [(src, 0, 1)], [(nm, 0, 1)])
-    ts(T.ev[:, :], T.od[:, :], -1.0, 1.0, MUL, ADD, [("od", 0, 1)], [("ev", 0, 1)])
     ts(T.lama[:, :], T.pq[:, :], 512.0, 512.0, MUL, ADD, [("pq", 0, 1)], [("lama", 0, 1)])
     ts(T.lam[:, :], T.pl[:, :], 512.0, T.lama[:, 0:1], MUL, ADD, [("pl", 0, 1), ("lama", 0, 1)], [("lam", 0, 1)])
     for nm, c in (("lamb", -512.0), ("lams", -256.0)):
         ts(T[nm][:, :], T.lam[:, :], c, None, ADD, None, [("lam", 0, 1)], [(nm, 0, 1)])
-    fill("et", 0, 2048, 0.0)
-    for b in range(4):
-        tc(T.et[:, 512 * b + b:512 * b + 512:4], T.ident[:, :], [("ident", 0, 128)], [("et", 512 * b, 512 * b + 512)])
+    fill("ar1", E, E + 16, TOP[1])
+    fill("ar2", E, E + 16, TOP[2])
+    fill("lr", E, E + 16, 0.5)
+    fill("ks", 0, 8, -9.0e6)
     quant("qx0", "sx0", "xt0", 0, 128, xr(0, 0, 128))
     send(0)
     op("g", [("ones", 0, 512)], [("ga", 0, 512)], g.affine_select, T.ga[:, :], T.ones[:, :], [[-16, 8], [0, 64]], GE, 0.0, 0, 1)
     op("g", [("ga", 0, 512)], [("gt", 0, 512)], g.affine_select, T.gt[:, :], T.ga[:, :], [[16, 8], [0, 64]], GE, 0.0, 15, -1)
-    op("g", [], [("iom", 0, E)], g.iota, T.iom[:, :], [[1, E]], -192, 0, allow_small_or_imprecise_dtypes=True)
     op("g", [], [("iof", 0, E)], g.iota, T.iof[:, :], [[1, E]], 0, 0, allow_small_or_imprecise_dtypes=True)
+    op("g", [], [("iom", 0, E)], g.iota, T.iom[:, :], [[1, E]], -192, 0, allow_small_or_imprecise_dtypes=True)
     quant("qu", "su", "ut", 0, 128, [("ut", 0, 128)])
     op("v", [("qu", 0, 128), ("uo16", 0, 16)], [("qur", 0, 256)], g.vector.tensor_copy,
        T.qur[:, 0:256].bitcast(dt.uint32), T.qu[:, 0:128].bitcast(dt.uint32).indirect(T.uo16[:, 0:16]))
-    act(V("hl", 2, 1920, 4), V("ones", 0, 480), COPY, [("ones", 0, 512)], [("hl", 2, 3)], scale=0.0)
-    act(V("hl", 3, 1920, 4), V("ones", 0, 480), COPY, [("ones", 0, 512)], [("hl", 3, 4)], scale=0.0)
+    act(V("hl", 2, 4 * E, 4), V("ones", 0, E), COPY, [("ones", 0, 512)], [("hl", 2, 3)], scale=0.0)
+    act(V("hl", 3, 4 * E, 4), V("ones", 0, E), COPY, [("ones", 0, 512)], [("hl", 3, 4)], scale=0.0)
     op("a", [("qu", 0, 128), ("uo16", 0, 16)], [("qurs", 0, 256)], g.scalar.activation,
        T.sur[:, 0:256], T.su[:, 0:128].indirect(T.uo16[:, 0:16]), COPY)
-    for b in range(2):
-        act(V("hl", b, 64, 4), V("ones", 0, 16), COPY, [("ones", 0, 512)], [("hl", 4 + b, 5 + b)], scale=0.0)
-        act(V("hl", 4 * (OFF + E) + b, 1920, 4), V("ones", 0, 16), COPY, [("ones", 0, 512)], [("hl", 6 + b, 7 + b)], scale=0.0)
     quant("qx0", "sx0", "xt0", 128, C, xr(0, 128, C))
-    quant("qe", "se", "et", 0, 512, [("et", 0, 2048)])
     for b in range(4):
-        act(V("vp", E * b, E * b + C), V("xt0", b, 4 * C, 4), COPY, [("x0_%d" % b, 0, C)], [("vp%d" % b, 0, C)], scale=0.5)
+        act(V("vp", E * b, E * b + C), V("xt0", b, 4 * C, 4), COPY, [("x0_%d" % b, 0, C)], [("vp%d" % b, 0, C)], scale=2.0 ** -6)
     waits("t", [("qurs", 0, 256)], [])
 
-    def wrap(row, reg, ta, tb, out):
-        op("v", reg, [(ta, 0, E)], g.vector.transpose, V(ta, 0, E), row(OFF, OFF + E))
-        op("v", reg, [(tb, 0, E)], g.vector.transpose, V(tb, 0, E + 32), row(0, E + 32))
-        tt(V("o1", 0, 28), V(ta, 0, E, 16), V("ma", 0, 28), MUL, [(ta, 0, E), ("ma", 0, 2)], [("o1", 0, 28)])
-        tt(V("o2", 0, 28), V(tb, 16, E + 16, 16), V("mb", 0, 28), MUL, [(tb, 0, E), ("mb", 0, 2)], [("o2", 0, 28)])
-        tt(V(out, 0, 28), V("o1", 0, 28), V("o2", 0, 28), ADD, [("o1", 0, 28), ("o2", 0, 28)], [(out, 0, 28)])
+    def wrap(row, reg, a, b):
+        scan(V(a, 0, E), row, V("dm", 0, E), 0.0, ADD, MUL, reg + [("dm", 0, E)], [(a, 0, E)])
+        scan(V(b, 0, E), V("kp", 0, E), V(a, 0, E), 0.0, MUL, ADD, [("kp", 0, E), (a, 0, E)], [(b, 0, E)])
 
     def words0(k, sl, sh, lo, hi, klo, khi):
         ts(V("t1", lo, hi), bank(k, sl, sh), 0.0, 1024.0, GT, MUL, [("b%d" % k, 0, 1)], [("t1", lo, hi)])
@@ -201,18 +195,16 @@ def rank_program(g, core, T, topo):
     def words(t, k, sl, sh, lo, hi):
         d = 2 ** t
         ar, klo, khi = "ar%d" % t, max(lo - d, 0), hi if hi == E else hi - d
-        unit, fac = ((512.0, 41.0), (1.0, 3281.0))[t - 1]
-        ts(V(ar, lo, hi), bank(k, sl, sh), 0.0, unit, GT, MUL, [("b%d" % k, 0, 1)], [(ar, lo, hi)])
-        ts(V("al", klo, khi), V(ar, klo, khi), fac, None, MUL, None, [(ar, klo, khi)], [("al", klo, khi)])
-        tt(V("ag", klo, khi), V("al", klo, khi), V("g1", klo, khi), ADD, [("al", klo, khi), ("g1", klo, khi)], [("ag", klo, khi)])
-        tt(V("kr", OFF + klo, OFF + khi), V("ag", klo, khi), V(ar, klo + d, khi + d), ADD,
-           [("ag", klo, khi), (ar, klo + d, khi + d)], [("kr", OFF + klo, OFF + khi)])
+        ts(V(ar, lo, hi), bank(k, sl, sh), 0.0, TOP[t], GT, ADD, [("b%d" % k, 0, 1)], [(ar, lo, hi)])
+        ts(V("al", klo, khi), V(ar, klo, khi), TOP[t], FAC[t], SUB, MUL, [(ar, klo, khi)], [("al", klo, khi)])
+        scan(V("ag", klo, khi), V("al", klo, khi), V("g1", klo, khi), 0.0, MAX, ADD, [("al", klo, khi), ("g1", klo, khi)], [("ag", klo, khi)])
+        scan(V("kr", klo, khi), V(ar, klo + d, khi + d), V("ag", klo, khi), 0.0, MAX, ADD,
+             [("ag", klo, khi), (ar, klo + d, khi + d)], [("kr", klo, khi)])
         if t == NR - 1:
-            for o, e in ((0, 0.5), (E, -0.5)):
-                act(V("d2", o + klo, o + khi), V("kr", OFF + klo, OFF + khi), IDEN, [("kr", OFF + klo, OFF + khi)], [("d2", o + klo, o + khi)], bias=e)
+            act(V("kr", E + klo, E + khi), V("kr", klo, khi), IDEN, [("kr", klo, khi)], [("kr", E + klo, E + khi)], bias=-1.0)
 
-    K = V("kr", OFF, OFF + E)
-    KR = [("kr", OFF, OFF + E)]
+    K = V("kr", 0, E)
+    KR = [("kr", 0, E)]
 
     for t in range(NR):
         qx, sx = "qx%d" % t, "sx%d" % t
@@ -220,10 +212,13 @@ def rank_program(g, core, T, topo):
         if t == 0:
             mx(0, C, "qur", "sur", 0, qx, sx, 0, C)
             mx(1, C, "qur", "sur", 128, qx, sx, 0, C)
+            for b in range(4):
+                op("v", [("ft", 0, 516)], [("qe", 128 * b, 128 * b + 128)], g.vector.quantize_mx,
+                   V("qe", 128 * b, 128 * b + 128), V("se", 128 * b, 128 * b + 128), V("ft", 3 - b, 515 - b))
             words0(0, 0, C, 0, C, 0, C - 1)
-            for nm, a, b in (("ma", "ev", "od"), ("mb", "od", "ev")):
-                ts(V(nm, 0, 28, 2), V("ones", 0, 14), T[a][:, 0:1], None, MUL, None, [("ones", 0, 512), (a, 0, 1)], [(nm, 0, 1)])
-                ts(V(nm, 1, 28, 2), V("ones", 0, 14), T[b][:, 0:1], None, MUL, None, [("ones", 0, 512), (b, 0, 1)], [(nm, 1, 2)])
+            quant("qv", "sv", "vt", 0, 128, [("vt", 0, 128)])
+            ts(V("dm", 0, E), V("im", 0, E), T.pl[:, 0:1], None, EQ, None, [("im", 0, E), ("pl", 0, 1)], [("dm", 0, E)])
+            ts(V("kp", 0, E), V("im", 0, E), 0.0, None, GT, None, [("im", 0, E)], [("kp", 0, E)])
             mx(2, 128, "qur", "sur", 0, qx, sx, E - 128, E)
             mx(3, 128, "qur", "sur", 128, qx, sx, E - 128, E)
         else:
@@ -241,79 +236,72 @@ def rank_program(g, core, T, topo):
         ns = NS[t]
         nv = 28 - ns
         if t == 0:
-            act(V("s1", 0, E), V("er", 0, E), IDEN, [("er", 0, E)], [("s1", 0, E)], bias=512.0, scale=82.0)
-            act(V("s2", 0, E), V("er", 2, E + 2), COPY, [("er", 0, E + 16)], [("s2", 0, E)], scale=2.0)
-            for b in range(4):
-                act(V("x32", C * b, C * b + C), V("xt0", b, 4 * C, 4), COPY, [("x0_%d" % b, 0, C)], [("x32_%d" % b, 0, C)], scale=32.0)
+            act(V("ios", 0, E), V("iof", 0, E), COPY, [("iof", 0, E)], [("ios", 0, E)], scale=2.0 ** -9)
+            act(V("s1", 0, E), V("er", 0, E), IDEN, [("er", 0, E)], [("s1", 0, E)], bias=-TOP[1], scale=82.0 / 512.0)
+            act(V("s2", 0, E), V("er", 2, E + 2), IDEN, [("er", 0, E + 16)], [("s2", 0, E)], bias=1.0, scale=2.0 / 512.0)
             O = V("cb", 0, E)
             ts(V("cb", 0, E - 1), V("er", 0, E - 1), T.lam[:, 0:1], None, EQ, None, [("er", 0, E), ("lam", 0, 1)], [("cb", 0, 1)])
             ts(V("cb", E - 1, E), V("er", E - 1, E), T.lamb[:, 0:1], None, EQ, None, [("er", 0, E), ("lamb", 0, 1)], [("cb", 1, 2)])
             quant("qg", "sg", "gt", 0, 128, [("gt", 0, 512)])
             ts(T.first[:, :], T.acc[:, 0:1], 0.5, 31.0, MUL, ADD, [("acc", 0, 1)], [("first", 0, 1)])
-            op("v", [("cb", 0, 2), ("ones", 0, 512), ("first", 0, 1)], [("t1", 0, E)], g.vector.tensor_tensor_scan,
-               V("t1", 0, E), V("ones", 0, E), O, T.first[:, 0:1], MUL, ADD)
+            scan(V("t1", 0, E), V("ones", 0, E), O, T.first[:, 0:1], MUL, ADD, [("cb", 0, 2), ("ones", 0, 512), ("first", 0, 1)], [("t1", 0, E)])
             tc(V("t1", E - 1, E), T.first[:, 0:1], [("first", 0, 1)], [("t1", E - 1, E)])
             tt(V("t2", 0, E), V("t1", 0, E), O, MUL, [("t1", 0, E), ("cb", 0, 2)], [("t2", 0, E)])
             ts(V("w6", 0, E), V("t2", 0, E), 3072.0, None, ADD, None, [("t2", 0, E)], [("w6", 0, E)])
-            d0, d1 = V("hl", 4 * OFF, 4 * (OFF + E), 4), V("hl", 4 * OFF + 1, 4 * (OFF + E), 4)
+            d0, d1 = V("hl", 0, 4 * E, 4), V("hl", 1, 4 * E, 4)
             ts(d0, V("w6", 0, E), -3072.0, None, ADD, None, [("w6", 0, E)], [("hl", 0, 1)])
             tt(d1, V("t2", 0, E), d0, SUB, [("t2", 0, E), ("hl", 0, 1)], [("hl", 1, 2)])
-            quant("qh", "sh", "hl", 0, E + 32, [("hl", 0, 8)])
-            mx(3, E + 32, "qg", "sg", 0, "qh", "sh", 0, E + 32)
-            tt(V("g1", 0, E), V("s1", 0, E), V("iof", 0, E), ADD, [("s1", 0, E), ("iof", 0, E)], [("g1", 0, E)])
-            wrap(lambda lo, hi: bank(3, lo, hi), [("b3", 0, 1)], "ka", "kb", "p3")
-            ts(V("pos", 0, 28), V("p3", 0, 28), 192.0, None, ADD, None, [("p3", 0, 28)], [("pos", 0, 28)])
+            quant("qh", "sh", "hl", 0, E, [("hl", 0, 4)])
+            mx(3, E, "qg", "sg", 0, "qh", "sh", 0, E)
+            scan(V("ga1", 0, E), V("ios", 0, E), V("s1", 0, E), 0.0, MAX, ADD, [("ios", 0, E), ("s1", 0, E)], [("ga1", 0, E)])
+            wrap(bank(3, 0, E), [("b3", 0, 1)], "b1", "b2")
+            ts(V("pos", 0, 28), V("b2", 15, E, 16), 192.0, None, ADD, None, [("b2", 0, E)], [("pos", 0, 28)])
         else:
-            wrap(lambda lo, hi: V("kr", lo, hi), [("kr", 0, E + 32)], "ka", "kb", "own")
-
-            def row(c):
-                if not last:
-                    return K, KR
-                return V("d2", 16 * c + 16, 16 * c + 16 + E), [("d2", 16 * c + 16, 16 * c + 16 + E)]
-
-            for c in range(ns):
-                v, r = row(c)
-                j = c % 4
-                act(V("junk", E * j, E * j + E), v, SIGN, r + [("own", 0, 28)], [("junk%d" % j, 0, 1), ("acc", c, c + 1)],
-                    bias=T.own[:, c:c + 1], scale=-1.0, accum_out=T.acc[:, c:c + 1])
+            wrap(K, KR, "x1", "x2")
             if last:
-                for q in range(1, 16):
-                    o = 112 * (q // 4) + q % 4
-                    tt(V("eq", o, 112 * (q // 4) + 112, 4), V("kr", OFF + q, OFF + E, 16), V("own", 0, 28), EQ, KR + [("own", 0, 28)], [("eq", 1000 + q, 1001 + q)])
-                quant("qq", "sq", "eq", 0, 212, [("eq", 0, 1016)])
-                for k in range(4):
-                    mx(3, 128, "qc", "cs", 128 * k, "qq", "sq", 28 * k, 28 * k + 128, k == 0, k == 3)
+                ts(V("own", 0, 28), V("x2", 15, E, 16), -0.5, None, ADD, None, [("x2", 0, E)], [("own", 0, 28)])
+                own = lambda c: (T.own[:, c:c + 1], [("own", 0, 28)])
+                row = lambda c: (V("kr", 16 * c + 16, 16 * c + 16 + E), [("kr", 16 * c + 16, 16 * c + 16 + E)])
+            else:
+                own = lambda c: (T.x2[:, 16 * c + 15:16 * c + 16], [("x2", 0, E)])
+                row = lambda c: (K, KR)
+            for c in range(ns):
+                (v, r), (o, ro) = row(c), own(c)
+                j = c % 4
+                act(V("junk", E * j, E * j + E), v, SIGN, r + ro, [("junk%d" % j, 0, 1), ("acc", c, c + 1)],
+                    bias=o, scale=-1.0, accum_out=T.acc[:, c:c + 1])
+            if last:
+                tt(V("eq", 0, E), K, V("x2", 0, E), EQ, KR + [("x2", 0, E)], [("eq", 0, E)])
+                scan(V("te", 0, E), V("kp", 0, E), V("eq", 0, E), 0.0, MUL, ADD, [("kp", 0, E), ("eq", 0, E)], [("te", 0, E)])
+                ts(V("ti", ns, 28), V("te", 16 * ns + 15, E, 16), -1.0, -192.0, MUL, ADD, [("te", 0, E)], [("ti", ns, 28)])
+                ts(V("tj", 0, ns), V("te", 15, 16 * ns, 16), -2.0, float(E), MUL, ADD, [("te", 0, E)], [("tj", 0, ns)])
             for k in range(nv):
-                v, r = row(ns + k)
-                ts(V("cb", E * k, E * k + E), v, T.own[:, ns + k:ns + k + 1], None, LT, None, r + [("own", 0, 28)], [("cb", k, k + 1)])
+                (v, r), (o, ro) = row(ns + k), own(ns + k)
+                ts(V("cb", E * k, E * k + E), v, o, None, LT, None, r + ro, [("cb", k, k + 1)])
             for k in range(nv):
-                op("v", [("cb", k, k + 1)], [("sc", k, k + 1)], g.vector.tensor_tensor_scan, V("sc", 224 * k, 224 * k + 224),
-                   V("cb", E * k, E * k + 224), V("cb", E * k + 224, E * k + E), -192.0, ADD, ADD)
-            cnt = V("sc", 223, 224 * nv, 224)
+                ini, ri = (T.ti[:, ns + k:ns + k + 1], [("ti", ns, 28)]) if last else (-192.0, [])
+                scan(V("sc", 224 * k, 224 * k + 224), V("cb", E * k, E * k + 224), V("cb", E * k + 224, E * k + E), ini, ADD, ADD,
+                     ri + [("cb", k, k + 1)], [("sc", k, k + 1)])
+            ts(V("pos", ns, 28), V("sc", 223, 224 * nv, 224), 192.0, None, ADD, None, [("sc", 0, nv)], [("pos", ns, 28)])
             if not last:
-                ts(V("pos", ns, 28), cnt, 192.0, None, ADD, None, [("sc", 0, nv)], [("pos", ns, 28)])
                 ts(V("pos", 0, ns), V("acc", 0, ns), 0.5, 223.5, MUL, ADD, [("acc", 0, ns)], [("pos", 0, ns)])
             else:
-                ts(V("posf", ns, 28), cnt, 191.0, None, ADD, None, [("sc", 0, nv)], [("posf", ns, 28)])
-                ts(V("posf", 0, ns), V("acc", 0, ns), 0.5, 223.0, MUL, ADD, [("acc", 0, ns)], [("posf", 0, ns)])
-                tt(V("posg", 0, 28), V("posf", 0, 28), bank(3, 0, 28), SUB, [("posf", 0, 28), ("b3", 0, 1)], [("posg", 0, 28)])
-                tc(V("pos", 0, 28), V("posg", 0, 28), [("posg", 0, 28)], [("pos", 0, 28)])
-        tc(V("ordr", OFF, OFF + E).indirect(V("pos", 0, 28)), V("iom", 0, E), [("iom", 0, E), ("pos", 0, 28)], [("ordr", OFF, OFF + E)])
-        wrap(lambda lo, hi: V("ordr", lo, hi), [("ordr", 0, E + 32)], "oa", "ob", "p3")
-        ts(V("ordl", 0, 28), V("p3", 0, 28), 192.0, None, ADD, None, [("p3", 0, 28)], [("ordl", 0, 28)])
-        for b in range(4):
+                tt(V("posf", 0, ns), V("acc", 0, ns), V("tj", 0, ns), ADD, [("acc", 0, ns), ("tj", 0, ns)], [("posf", 0, ns)])
+                ts(V("pos", 0, ns), V("posf", 0, ns), 0.5, None, MUL, None, [("posf", 0, ns)], [("pos", 0, ns)])
+        tc(V("ordr", 0, E).indirect(V("pos", 0, 28)), V("iom", 0, E), [("iom", 0, E), ("pos", 0, 28)], [("ordr", 0, E)])
+        wrap(V("ordr", 0, E), [("ordr", 0, E)], "b1", "b2")
+        ts(V("ordl", 0, 28), V("b2", 15, E, 16), 192.0, None, ADD, None, [("b2", 0, E)], [("ordl", 0, 28)])
+        for b in range(3):
             act(V("vs", E * b, E * b + E), V("vp", E * b, E * b + E).indirect(V("ordl", 0, 28)), COPY,
                 [("vp%d" % b, 0, E), ("ordl", 0, 28)], [("vs%d" % b, 0, 1)])
+        tc(V("vs", 3 * E, 4 * E), V("vp", 3 * E, 4 * E).indirect(V("ordl", 0, 28)), [("vp3", 0, E), ("ordl", 0, 28)], [("vs3", 0, 1)])
+        if t == 1:
+            scan(V("lr", 0, E), V("ios", 0, E), K, 0.0, MAX, SUB, [("ios", 0, E)] + KR, [("lr", 0, E)])
+            act(V("s1", 0, E), V("lr", 0, E), IDEN, [("lr", 0, E)], [("s1", 0, E)], bias=0.5 - TOP[2] - CENTER, scale=-6562.0)
+            act(V("s2", 0, E), V("lr", 4, E + 4), IDEN, [("lr", 0, E + 16)], [("s2", 0, E)], bias=1.0, scale=-2.0)
         if last:
             act(V("ks", 1, 1 + E), K.indirect(V("ordl", 0, 28)), COPY, KR + [("ordl", 0, 28)], [("ks", 1, 1 + E)])
-        if t == 0:
-            tt(V("g1", 0, E), V("g1", 0, E), V("s2", 0, E), ADD, [("g1", 0, E), ("s2", 0, E)], [("g1", 0, E)])
-        elif t == 1:
-            fill("lr", E, E + 16, -256.0)
-            tt(V("lr", 0, E), K, V("iof", 0, E), SUB, KR + [("iof", 0, E)], [("lr", 0, E)])
-            act(V("s1", 0, E), V("lr", 0, E), IDEN, [("lr", 0, E)], [("s1", 0, E)], bias=1.0 - CENTER, scale=6562.0 / 512.0)
-            act(V("s2", 0, E), V("lr", 4, E + 4), COPY, [("lr", 0, E + 16)], [("s2", 0, E)], scale=1.0 / 256.0)
-        for b in range(4):
+        for b in (3, 0, 1, 2):
             o = E * b
             tt(V("mm", o + 1, o + E - 1), V("vs", o, o + E - 2), V("vs", o + 2, o + E), MAX, [("vs%d" % b, 0, 1)], [("mm%d" % b, 0, 1)])
         ends = [("vs%d" % b, 0, 1) for b in range(4)]
@@ -329,80 +317,62 @@ def rank_program(g, core, T, topo):
             for b in range(4):
                 mx(b0 + b, hi - lo, "qw", "sw", 128 * b, "qz", "sz", lo, hi)
 
-        xn = "xt%d" % (t + 1)
+        xo, xn = "xt%d" % t, "xt%d" % (t + 1)
 
         def update(lo, hi, b0):
             for b in range(4):
-                r = [("x32_%d" % b, lo, hi)]
-                tt(V("x32", C * b + lo, C * b + hi), bank(b0 + b, 0, hi - lo), V("x32", C * b + lo, C * b + hi), ADD, [("b%d" % (b0 + b), 0, 1)] + r, r)
-            for b in range(4):
-                o, i, W = V(xn, 4 * lo + b, 4 * hi, 4), V("x32", C * b + lo, C * b + hi), [("x%d_%d" % (t + 1, b), lo, hi)]
-                if b < 3:
-                    act(o, i, COPY, [("x32_%d" % b, lo, hi)], W, scale=0.03125)
-                else:
-                    ts(o, i, 0.03125, None, MUL, None, [("x32_%d" % b, lo, hi)], W)
+                tt(V(xn, 4 * lo + b, 4 * hi, 4), bank(b0 + b, 0, hi - lo), V(xo, 4 * lo + b, 4 * hi, 4), ADD,
+                   [("b%d" % (b0 + b), 0, 1), ("x%d_%d" % (t, b), lo, hi)], [("x%d_%d" % (t + 1, b), lo, hi)])
 
         def planes(lo, hi):
             for b in range(4):
-                act(V("vp", E * b + lo, E * b + hi), V("x32", C * b + lo, C * b + hi), COPY, [("x32_%d" % b, lo, hi)], [("vp%d" % b, lo, hi)], scale=2.0 ** -6)
+                act(V("vp", E * b + lo, E * b + hi), V(xn, 4 * lo + b, 4 * hi, 4), COPY, [("x%d_%d" % (t + 1, b), lo, hi)], [("vp%d" % b, lo, hi)], scale=2.0 ** -6)
 
         qn, sn = "qx%d" % (t + 1), "sx%d" % (t + 1)
-        for b in range(4):
-            fused(b, 0, 128)
-        product(0, 128, 0)
-        fused(0, 128, C)
-        update(0, 128, 0)
-        fused(1, 128, C)
-        quant(qn, sn, xn, 0, 128, xr(t + 1, 0, 128))
+        cut = 256 if last else 128
+        for b in (3, 0, 1, 2):
+            fused(b, 0, cut)
+        product(0, cut, 0)
+        fused(0, cut, C)
+        update(0, cut, 0)
+        fused(1, cut, C)
+        quant(qn, sn, xn, 0, cut, xr(t + 1, 0, cut))
         if not last:
             send(t + 1)
             mx(0, 128, "qur", "sur", 0, qn, sn, 0, 128)
             planes(0, 128)
         else:
-            dma("s", "dca", [(qn, 0, 128)], [], T.oc[:, 0:512], V(qn, 0, 128).bitcast(dt.uint8))
-            mx(0, 128, "qv", "sv", 0, qn, sn, 0, 128)
-            act(V("yr", 0, 128), bank(0, 0, 128), COPY, [("b0", 0, 1)], [("yr", 0, 128)])
-            dma("s", "dya", [("yr", 0, 128)], [], T.y[:, 0:128], T.yr[:, 0:128])
-        fused(2, 128, C)
-        fused(3, 128, C)
-        product(128, C, 4)
+            dma("s", "dca", [(qn, 0, cut)], [], T.oc[:, 0:4 * cut], V(qn, 0, cut).bitcast(dt.uint8))
+            mx(0, cut, "qv", "sv", 0, qn, sn, 0, cut)
+            act(V("yr", 0, cut), bank(0, 0, cut), COPY, [("b0", 0, 1)], [("yr", 0, cut)])
+            dma("s", "dya", [("yr", 0, cut)], [], T.y[:, 0:cut], T.yr[:, 0:cut])
+        fused(2, cut, C)
+        fused(3, cut, C)
+        product(cut, C, 4)
         if t == 0:
-            fill("ar1", E, E + 16, 0.0)
-            fill("ar2", E, E + 16, 0.0)
-            for lo, hi in ((0, OFF), (OFF + E, E + 32)):
-                fill("kr", lo, hi, 0.0)
-            fill("eq", 0, 848, 0.0)
-            ts(T.behind[:, :], T.qi[:, :], T.pl[:, 0:1], 2.0, GT, MUL, [("qi", 0, 16), ("pl", 0, 1)], [("behind", 0, 16)])
+            scan(V("g1", 0, E), V("s2", 0, E), V("ga1", 0, E), 0.0, MAX, ADD, [("s2", 0, E), ("ga1", 0, E)], [("g1", 0, E)])
         elif t == 1:
-            tt(V("g1", 0, E), V("s1", 0, E), V("s2", 0, E), ADD, [("s1", 0, E), ("s2", 0, E)], [("g1", 0, E)])
+            scan(V("g1", 0, E), V("s2", 0, E), V("s1", 0, E), 0.0, MAX, ADD, [("s1", 0, E), ("s2", 0, E)], [("g1", 0, E)])
         else:
             tt(V("eqs", 0, E), V("ks", 1, E + 1), V("ks", 0, E), EQ, [("ks", 0, E + 1)], [("eqs", 0, E)])
-            op("v", [("ones", 0, 512), ("eqs", 0, E)], [("rr", 0, E)], g.vector.tensor_tensor_scan, V("rr", 0, E), V("ones", 0, E), V("eqs", 0, E), 0.0, ADD, MUL)
-        update(128, C, 4)
-        quant(qn, sn, xn, 128, C, xr(t + 1, 128, C))
-        if t == 1:
-            quant("qc", "cs", "ct", 0, 512, [("ct", 0, 16)])
-            quant("qv", "sv", "vt", 0, 128, [("vt", 0, 128)])
-            fill("ks", 0, 8, -9.0e6)
+            scan(V("rr", 0, E), V("ones", 0, E), V("eqs", 0, E), 0.0, ADD, MUL, [("ones", 0, 512), ("eqs", 0, E)], [("rr", 0, E)])
+            scan(V("lw", 0, E), V("iof", 0, E), V("rr", 0, E), 0.0, MAX, SUB, [("iof", 0, E), ("rr", 0, E)], [("lw", 0, E)])
+        update(cut, C, 4)
+        quant(qn, sn, xn, cut, C, xr(t + 1, cut, C))
         if not last:
             words(t + 1, 0, 0, 128, 0, 128)
             planes(128, C)
-            if t == 0:
-                for q in range(16):
-                    o = 512 * (q // 4)
-                    act(T.ct[:, o + q % 4:o + 512:4], T.ident[:, :], COPY, [("ident", 0, 128), ("behind", 0, 16)], [("ct", q, q + 1)], scale=T.behind[:, q:q + 1])
         else:
-            tt(V("lw", 0, E), V("iof", 0, E), V("rr", 0, E), SUB, [("iof", 0, E), ("rr", 0, E)], [("lw", 0, E)])
+            act(V("lvr", 0, E), V("lw", 0, E).indirect(V("pos", 0, 28)), COPY, [("lw", 0, E), ("pos", 0, 28)], [("lvr", 0, E)])
+            dma("s", "dlv", [("lvr", 0, E)], [], T.lv[:, :], T.lvr[0:128:16, 0:E])
 
     q, s = "qx%d" % NR, "sx%d" % NR
-    mx(1, C - 128, "qv", "sv", 0, q, s, 128, C)
-    dma("s", "dcb", [(q, 128, C)], [], T.oc[:, 512:1536], V(q, 128, C).bitcast(dt.uint8))
+    mx(1, C - cut, "qv", "sv", 0, q, s, cut, C)
+    dma("s", "dcb", [(q, cut, C)], [], T.oc[:, 4 * cut:4 * C], V(q, cut, C).bitcast(dt.uint8))
     for k in range(4):
         dma("s", "ds%d" % k, [(q, 0, C)], [], T.osc[4 * k:4 * k + 4, 0:C], T[s][32 * k:32 * k + 4, 0:C])
-    act(V("yr", 128, C), bank(1, 0, C - 128), COPY, [("b1", 0, 1)], [("yr", 128, C)])
-    dma("a", "dyb", [("yr", 128, C)], [], T.y[:, 128:C], T.yr[:, 128:C])
-    act(V("lvr", 0, E), V("lw", 0, E).indirect(V("pos", 0, 28)), COPY, [("lw", 0, E), ("pos", 0, 28)], [("lvr", 0, E)])
-    dma("s", "dlv", [("lvr", 0, E)], [], T.lv[:, :], T.lvr[0:128:16, 0:E])
+    act(V("yr", cut, C), bank(1, 0, C - cut), COPY, [("b1", 0, 1)], [("yr", cut, C)])
+    dma("a", "dyb", [("yr", cut, C)], [], T.y[:, cut:C], T.yr[:, cut:C])
     for sem in count:
         g.wait_ge(T.sem[sem], count[sem])
     for sem in DMAS:

from concourse.mybir import dt, AluOpType, ActivationFunctionType

C, H, E, NR = 384, 64, 448, 3
NS = (0, 16, 18)

SCRATCH = {}
for _k, _n in (("qu", 128), ("qur", 256), ("qv", 128), ("qw", 512), ("qe", 512), ("qz", C), ("qg", 128), ("qh", E)):
    SCRATCH[_k] = ("sbuf", [128, _n], "float8_e4m3fn_x4")
    SCRATCH["s" + _k[1:]] = ("sbuf", [128, _n], "uint8")
for _k, _n in (("ut", 512), ("vt", 512), ("fv", 516), ("ft", 516), ("gt", 512), ("ga", 512), ("hl", 4 * E), ("zt", 4 * C), ("vp", 4 * E),
               ("vs", 4 * E), ("mm", 4 * E), ("iom", E), ("im", E), ("dm", E), ("kp", E), ("ones", 512), ("t1", E), ("t2", E),
               ("w5", E + 16), ("w6", E), ("er", E + 16), ("junk", 4 * E), ("cb", 16 * E), ("sc", 8 * E),
               ("ordr", E), ("b1", E), ("b2", E), ("eq", E), ("te", E), ("eqs", E), ("sg1", E)):
    SCRATCH[_k] = ("sbuf", [128, _n], "bfloat16")
for _k, _n in (("iof", E), ("ios", E), ("pl", 1), ("pq", 1), ("lama", 1), ("lam", 1), ("lamb", 1), ("lams", 1), ("first", 1),
               ("ar1", E + 16), ("ar2", E + 16), ("lr", E + 16), ("al", E), ("ag", E), ("ga1", E), ("g1", E), ("s1", E), ("s2", E),
               ("kr", 2 * E), ("x1", E), ("x2", E), ("own", 28), ("acc", 28), ("ti", 28), ("tj", 28), ("posf", 28),
               ("ks", E + 16), ("rr", E), ("lw", E), ("lvr", E), ("yr", C)):
    SCRATCH[_k] = ("sbuf", [128, _n], "float32")
for _k, _n in (("uo", 16), ("pin", 1), ("pla", 1), ("plq", 1)):
    SCRATCH[_k] = ("sbuf", [128, _n], "int32")
for _k, _n in (("uo16", 16), ("pos", 28), ("ordl", 28)):
    SCRATCH[_k] = ("sbuf", [128, _n], "uint16")
SCRATCH["ps"] = ("psum", [128, 4096], "float32")
for _t in range(NR + 1):
    SCRATCH["xt%d" % _t] = ("sbuf", [128, 4 * C], "bfloat16")
    SCRATCH["qx%d" % _t] = ("sbuf", [128, E], "float8_e4m3fn_x4")
    SCRATCH["sx%d" % _t] = ("sbuf", [128, E], "uint8")
DMAS = ["dxa", "dxb", "du", "dv", "dwc", "dws", "dlv", "dya", "dyb", "dca", "dcb"] + ["ds%d" % k for k in range(4)]
SEMAPHORES = ["vec", "act", "ten", "pool", "left"] + ["arr%d" % t for t in range(NR)] + DMAS

ADD, SUB, MUL, MAX = AluOpType.add, AluOpType.subtract, AluOpType.mult, AluOpType.max
GT, LT, GE, EQ = AluOpType.is_gt, AluOpType.is_lt, AluOpType.is_ge, AluOpType.is_equal
COPY, IDEN, SIGN = ActivationFunctionType.Copy, ActivationFunctionType.Identity, ActivationFunctionType.Sign
TOP = (None, 2048.0, 5381000.5)
CENTER = 5380840.0
FAC = (None, 41.0, 3281.0)


def rank_program(g, core, T, topo):
    rank = T.rank_of(core)
    if rank is None:
        return
    n = len(T.cores)
    prev, nxt = T.cores[(rank - 1) % n], T.cores[(rank + 1) % n]

    def send_engines(src, dst):
        return topo.engines(src, dst)[:8]

    queue = {"v": g.vector, "a": g.scalar, "t": g.tensor, "g": g, "s": g.sync}
    semof = {"v": "vec", "a": "act", "t": "ten", "g": "pool"}
    count = {"vec": 0, "act": 0, "ten": 0, "pool": 0}
    seen = {q: {} for q in queue}
    hist = {}

    def waits(q, reads, writes):
        need = {}
        for regs, isw in ((reads, False), (writes, True)):
            for name, lo, hi in regs:
                for l, h, w, oq, sem, val in hist.get(name, ()):
                    if l < hi and lo < h and (w or isw):
                        if oq == q and isw and not w:
                            continue
                        need[sem] = max(need.get(sem, 0), val)
        for sem in sorted(need):
            if seen[q].get(sem, 0) < need[sem]:
                queue[q].wait_ge(T.sem[sem], need[sem])
                seen[q][sem] = need[sem]

    def note(q, reads, writes, sem, val):
        for name, lo, hi in writes:
            hist[name] = [e for e in hist.get(name, ()) if not (lo <= e[0] and e[1] <= hi)] + [(lo, hi, True, q, sem, val)]
        for name, lo, hi in reads:
            hist.setdefault(name, []).append((lo, hi, False, q, sem, val))

    def op(q, reads, writes, fn, *args, **kw):
        waits(q, reads, writes)
        sem = semof[q]
        fn(*args, **kw).then_inc(T.sem[sem], 1)
        count[sem] += 1
        note(q, reads, writes, sem, count[sem])

    def dma(q, sem, reads, writes, out, in_):
        waits(q, reads, writes)
        queue[q].dma_start(out, in_).then_inc(T.sem[sem], 16)
        note("dma", reads, writes, sem, 16)

    def V(name, lo, hi, step=1):
        return T[name][:, lo:hi] if step == 1 else T[name][:, lo:hi:step]

    def tt(out, a, b, o, R, W):
        op("v", R, W, g.vector.tensor_tensor, out, a, b, o)

    def ts(out, a, s1, s2, o0, o1, R, W):
        if o1 is None:
            op("v", R, W, g.vector.tensor_scalar, out, a, s1, None, o0)
        else:
            op("v", R, W, g.vector.tensor_scalar, out, a, s1, s2, o0, o1)

    def tc(out, in_, R, W):
        op("v", R, W, g.vector.tensor_copy, out, in_)

    def scan(out, a, b, ini, o0, o1, R, W):
        op("v", R, W, g.vector.tensor_tensor_scan, out, a, b, ini, o0, o1)

    def act(out, in_, f, R, W, **kw):
        op("a", R, W, g.scalar.activation, out, in_, f, **kw)

    def fill(name, lo, hi, c):
        op("v", [], [(name, lo, hi)], g.vector.memset, V(name, lo, hi), c)

    def quant(codes, plane, src, lo, hi, R):
        op("v", R, [(codes, lo, hi)], g.vector.quantize_mx, V(codes, lo, hi), V(plane, lo, hi), V(src, 4 * lo, 4 * hi))

    def mx(bank, cols, l, ls, llo, r, rs, rlo, rhi, start=True, stop=True):
        op("t", [(l, llo, llo + 128), (r, rlo, rhi)], [("b%d" % bank, 0, 512)], g.tensor.matmul_mx,
           T.ps[:, 512 * bank:512 * bank + cols], V(l, llo, llo + 128), V(ls, llo, llo + 128),
           V(r, rlo, rhi), V(rs, rlo, rhi), start, stop)

    def bank(k, lo, hi):
        return T.ps[:, 512 * k + lo:512 * k + hi]

    def send(t):
        waits("g", [("qx%d" % t, 0, H)], [])
        rid, pid = topo.addr(prev)[0], topo.addr(prev)[1]
        m = 0
        for e in send_engines(core, prev):
            m |= 1 << e
        q, s = "qx%d" % t, "sx%d" % t
        g.remote_dma(V(q, C, E).bitcast(dt.uint8), V(q, 0, H).bitcast(dt.uint8), T.sem["arr%d" % t], T.sem.left, pid, rid, m)
        g.remote_dma(V(s, C, E), V(s, 0, H), T.sem["arr%d" % t], T.sem.left, pid, rid, m)
        note("remote", [], [(q, C, E)], "arr%d" % t, 2 * len(send_engines(nxt, core)))

    xr = lambda t, lo, hi: [("x%d_%d" % (t, b), lo, hi) for b in range(4)]
    dma("s", "dxa", [], xr(0, 0, 128), T.xt0[:, 0:512], T.x[:, 0:512])
    dma("a", "du", [], [("ut", 0, 128)], T.ut[:, :], T.u[:, :])
    dma("s", "dxb", [], xr(0, 128, C), T.xt0[:, 512:1536], T.x[:, 512:1536])
    dma("s", "dwc", [], [("qw", 0, 512)], T.qw[:, 0:512].bitcast(dt.uint8), T.wc[:, :])
    dma("s", "dws", [], [("qw", 0, 512)], T.sw[:, :], T.ws[:, :])
    dma("a", "dv", [], [("vt", 0, 128)], T.vt[:, :], T.v[:, :])
    hist["qw"] = [(0, 512, True, "dma", "dwc", 16), (0, 512, True, "dma", "dws", 16)]
    fill("fv", 0, 516, 2.0 ** -6)
    op("g", [], [("uo", 0, 16)], g.iota, T.uo[:, :], [[1, 2], [16, 8]], 0, 0)
    op("g", [], [("pin", 0, 1)], g.iota, T.pin[:, :], [[0, 1]], 0, 1)
    op("g", [("fv", 0, 516)], [("ft", 0, 516)], g.affine_select, T.ft[:, :], T.fv[:, :], [[-1, 516]], EQ, 0.0, 3, 4)
    op("g", [], [("im", 0, E)], g.iota, T.im[:, :], [[0, 28], [1, 16]], 0, 0, allow_small_or_imprecise_dtypes=True)
    fill("ones", 0, 512, 1.0)
    fill("w5", E, E + 16, -512.0)
    fill("er", E, E + 16, -256.0)
    tc(T.uo16[:, :], T.uo[:, :], [("uo", 0, 16)], [("uo16", 0, 16)])
    for nm, a, b in (("pla", 15, None), ("plq", 2, 3)):
        if b is None:
            op("v", [("pin", 0, 1)], [(nm, 0, 1)], g.vector.tensor_scalar, T[nm][:, :], T.pin[:, :], a, b, AluOpType.bitwise_and)
        else:
            op("v", [("pin", 0, 1)], [(nm, 0, 1)], g.vector.tensor_scalar, T[nm][:, :], T.pin[:, :], a, b, AluOpType.logical_shift_right, AluOpType.bitwise_and)
    for nm, src in (("pl", "pla"), ("pq", "plq")):
        tc(T[nm][:, :], T[src][:, :], [(src, 0, 1)], [(nm, 0, 1)])
    ts(T.lama[:, :], T.pq[:, :], 512.0, 512.0, MUL, ADD, [("pq", 0, 1)], [("lama", 0, 1)])
    ts(T.lam[:, :], T.pl[:, :], 512.0, T.lama[:, 0:1], MUL, ADD, [("pl", 0, 1), ("lama", 0, 1)], [("lam", 0, 1)])
    for nm, c in (("lamb", -512.0), ("lams", -256.0)):
        ts(T[nm][:, :], T.lam[:, :], c, None, ADD, None, [("lam", 0, 1)], [(nm, 0, 1)])
    fill("ar1", E, E + 16, TOP[1])
    fill("ar2", E, E + 16, TOP[2])
    fill("lr", E, E + 16, 0.5)
    fill("ks", 0, 8, -9.0e6)
    quant("qx0", "sx0", "xt0", 0, 128, xr(0, 0, 128))
    send(0)
    op("g", [("ones", 0, 512)], [("ga", 0, 512)], g.affine_select, T.ga[:, :], T.ones[:, :], [[-16, 8], [0, 64]], GE, 0.0, 0, 1)
    op("g", [("ga", 0, 512)], [("gt", 0, 512)], g.affine_select, T.gt[:, :], T.ga[:, :], [[16, 8], [0, 64]], GE, 0.0, 15, -1)
    op("g", [], [("iof", 0, E)], g.iota, T.iof[:, :], [[1, E]], 0, 0, allow_small_or_imprecise_dtypes=True)
    op("g", [], [("iom", 0, E)], g.iota, T.iom[:, :], [[1, E]], -192, 0, allow_small_or_imprecise_dtypes=True)
    quant("qu", "su", "ut", 0, 128, [("ut", 0, 128)])
    op("v", [("qu", 0, 128), ("uo16", 0, 16)], [("qur", 0, 256)], g.vector.tensor_copy,
       T.qur[:, 0:256].bitcast(dt.uint32), T.qu[:, 0:128].bitcast(dt.uint32).indirect(T.uo16[:, 0:16]))
    act(V("hl", 2, 4 * E, 4), V("ones", 0, E), COPY, [("ones", 0, 512)], [("hl", 2, 3)], scale=0.0)
    act(V("hl", 3, 4 * E, 4), V("ones", 0, E), COPY, [("ones", 0, 512)], [("hl", 3, 4)], scale=0.0)
    op("a", [("qu", 0, 128), ("uo16", 0, 16)], [("qurs", 0, 256)], g.scalar.activation,
       T.sur[:, 0:256], T.su[:, 0:128].indirect(T.uo16[:, 0:16]), COPY)
    quant("qx0", "sx0", "xt0", 128, C, xr(0, 128, C))
    for b in range(4):
        act(V("vp", E * b, E * b + C), V("xt0", b, 4 * C, 4), COPY, [("x0_%d" % b, 0, C)], [("vp%d" % b, 0, C)], scale=2.0 ** -6)
    waits("t", [("qurs", 0, 256)], [])

    def wrap(row, reg, a, b):
        scan(V(a, 0, E), row, V("dm", 0, E), 0.0, ADD, MUL, reg + [("dm", 0, E)], [(a, 0, E)])
        scan(V(b, 0, E), V("kp", 0, E), V(a, 0, E), 0.0, MUL, ADD, [("kp", 0, E), (a, 0, E)], [(b, 0, E)])

    def words0(k, sl, sh, lo, hi, klo, khi):
        ts(V("t1", lo, hi), bank(k, sl, sh), 0.0, 1024.0, GT, MUL, [("b%d" % k, 0, 1)], [("t1", lo, hi)])
        ts(V("t2", lo, hi), bank(k + 1, sl, sh), 0.0, 512.0, GT, MUL, [("b%d" % (k + 1), 0, 1)], [("t2", lo, hi)])
        tt(V("w5", lo, hi), V("t1", lo, hi), V("t2", lo, hi), ADD, [("t1", lo, hi), ("t2", lo, hi)], [("w5", lo, hi)])
        ts(V("w6", klo, khi), V("w5", klo, khi), 5.0, 512.0, MUL, ADD, [("w5", klo, khi)], [("w6", klo, khi)])
        tt(V("er", klo, khi), V("w6", klo, khi), V("w5", klo + 1, khi + 1), ADD, [("w6", klo, khi), ("w5", klo + 1, khi + 1)], [("er", klo, khi)])

    def words(t, k, sl, sh, lo, hi):
        d = 2 ** t
        ar, klo, khi = "ar%d" % t, max(lo - d, 0), hi if hi == E else hi - d
        ts(V(ar, lo, hi), bank(k, sl, sh), 0.0, TOP[t], GT, ADD, [("b%d" % k, 0, 1)], [(ar, lo, hi)])
        ts(V("al", klo, khi), V(ar, klo, khi), TOP[t], FAC[t], SUB, MUL, [(ar, klo, khi)], [("al", klo, khi)])
        scan(V("ag", klo, khi), V("al", klo, khi), V("g1", klo, khi), 0.0, MAX, ADD, [("al", klo, khi), ("g1", klo, khi)], [("ag", klo, khi)])
        scan(V("kr", klo, khi), V(ar, klo + d, khi + d), V("ag", klo, khi), 0.0, MAX, ADD,
             [("ag", klo, khi), (ar, klo + d, khi + d)], [("kr", klo, khi)])
        if t == NR - 1:
            act(V("kr", E + klo, E + khi), V("kr", klo, khi), IDEN, [("kr", klo, khi)], [("kr", E + klo, E + khi)], bias=-1.0)

    K = V("kr", 0, E)
    KR = [("kr", 0, E)]

    for t in range(NR):
        qx, sx = "qx%d" % t, "sx%d" % t
        last = t == NR - 1
        if t == 0:
            mx(0, C, "qur", "sur", 0, qx, sx, 0, C)
            mx(1, C, "qur", "sur", 128, qx, sx, 0, C)
            for b in range(4):
                op("v", [("ft", 0, 516)], [("qe", 128 * b, 128 * b + 128)], g.vector.quantize_mx,
                   V("qe", 128 * b, 128 * b + 128), V("se", 128 * b, 128 * b + 128), V("ft", 3 - b, 515 - b))
            words0(0, 0, C, 0, C, 0, C - 1)
            quant("qv", "sv", "vt", 0, 128, [("vt", 0, 128)])
            ts(V("dm", 0, E), V("im", 0, E), T.pl[:, 0:1], None, EQ, None, [("im", 0, E), ("pl", 0, 1)], [("dm", 0, E)])
            ts(V("kp", 0, E), V("im", 0, E), 0.0, None, GT, None, [("im", 0, E)], [("kp", 0, E)])
            mx(2, 128, "qur", "sur", 0, qx, sx, E - 128, E)
            mx(3, 128, "qur", "sur", 128, qx, sx, E - 128, E)
        else:
            mx(1, E - 128, "qur", "sur", 0, qx, sx, 128, E)
        for b in range(4):
            mx(4 + b, 128, "qe", "se", 128 * b, qx, sx, E - 128, E)
        if t == 0:
            words0(2, 64, 128, C, E, C - 1, E)
            act(V("junk", 0, E), V("er", 0, E), SIGN, [("er", 0, E), ("lams", 0, 1)], [("junk0", 0, 1), ("acc", 0, 1)],
                bias=T.lams[:, 0:1], scale=-1.0, accum_out=T.acc[:, 0:1])
        else:
            words(t, 1, 0, E - 128, 128, E)
        for b in range(4):
            act(V("vp", E * b + C, E * b + E), bank(4 + b, 64, 128), COPY, [("b%d" % (4 + b), 0, 1)], [("vp%d" % b, C, E)])
        ns = NS[t]
        nv = 28 - ns
        if t == 0:
            act(V("ios", 0, E), V("iof", 0, E), COPY, [("iof", 0, E)], [("ios", 0, E)], scale=2.0 ** -9)
            act(V("s1", 0, E), V("er", 0, E), IDEN, [("er", 0, E)], [("s1", 0, E)], bias=-TOP[1], scale=82.0 / 512.0)
            act(V("s2", 0, E), V("er", 2, E + 2), IDEN, [("er", 0, E + 16)], [("s2", 0, E)], bias=1.0, scale=2.0 / 512.0)
            O = V("cb", 0, E)
            ts(V("cb", 0, E - 1), V("er", 0, E - 1), T.lam[:, 0:1], None, EQ, None, [("er", 0, E), ("lam", 0, 1)], [("cb", 0, 1)])
            ts(V("cb", E - 1, E), V("er", E - 1, E), T.lamb[:, 0:1], None, EQ, None, [("er", 0, E), ("lamb", 0, 1)], [("cb", 1, 2)])
            quant("qg", "sg", "gt", 0, 128, [("gt", 0, 512)])
            ts(T.first[:, :], T.acc[:, 0:1], 0.5, 31.0, MUL, ADD, [("acc", 0, 1)], [("first", 0, 1)])
            scan(V("t1", 0, E), V("ones", 0, E), O, T.first[:, 0:1], MUL, ADD, [("cb", 0, 2), ("ones", 0, 512), ("first", 0, 1)], [("t1", 0, E)])
            tc(V("t1", E - 1, E), T.first[:, 0:1], [("first", 0, 1)], [("t1", E - 1, E)])
            tt(V("t2", 0, E), V("t1", 0, E), O, MUL, [("t1", 0, E), ("cb", 0, 2)], [("t2", 0, E)])
            ts(V("w6", 0, E), V("t2", 0, E), 3072.0, None, ADD, None, [("t2", 0, E)], [("w6", 0, E)])
            d0, d1 = V("hl", 0, 4 * E, 4), V("hl", 1, 4 * E, 4)
            ts(d0, V("w6", 0, E), -3072.0, None, ADD, None, [("w6", 0, E)], [("hl", 0, 1)])
            tt(d1, V("t2", 0, E), d0, SUB, [("t2", 0, E), ("hl", 0, 1)], [("hl", 1, 2)])
            quant("qh", "sh", "hl", 0, E, [("hl", 0, 4)])
            mx(3, E, "qg", "sg", 0, "qh", "sh", 0, E)
            scan(V("ga1", 0, E), V("ios", 0, E), V("s1", 0, E), 0.0, MAX, ADD, [("ios", 0, E), ("s1", 0, E)], [("ga1", 0, E)])
            wrap(bank(3, 0, E), [("b3", 0, 1)], "b1", "b2")
            ts(V("pos", 0, 28), V("b2", 15, E, 16), 192.0, None, ADD, None, [("b2", 0, E)], [("pos", 0, 28)])
        else:
            wrap(K, KR, "x1", "x2")
            if last:
                ts(V("own", 0, 28), V("x2", 15, E, 16), -0.5, None, ADD, None, [("x2", 0, E)], [("own", 0, 28)])
                own = lambda c: (T.own[:, c:c + 1], [("own", 0, 28)])
                row = lambda c: (V("kr", 16 * c + 16, 16 * c + 16 + E), [("kr", 16 * c + 16, 16 * c + 16 + E)])
            else:
                own = lambda c: (T.x2[:, 16 * c + 15:16 * c + 16], [("x2", 0, E)])
                row = lambda c: (K, KR)
            for c in range(ns):
                (v, r), (o, ro) = row(c), own(c)
                j = c % 4
                act(V("junk", E * j, E * j + E), v, SIGN, r + ro, [("junk%d" % j, 0, 1), ("acc", c, c + 1)],
                    bias=o, scale=-1.0, accum_out=T.acc[:, c:c + 1])
            if last:
                tt(V("eq", 0, E), K, V("x2", 0, E), EQ, KR + [("x2", 0, E)], [("eq", 0, E)])
                scan(V("te", 0, E), V("kp", 0, E), V("eq", 0, E), 0.0, MUL, ADD, [("kp", 0, E), ("eq", 0, E)], [("te", 0, E)])
                ts(V("ti", ns, 28), V("te", 16 * ns + 15, E, 16), -1.0, -192.0, MUL, ADD, [("te", 0, E)], [("ti", ns, 28)])
                ts(V("tj", 0, ns), V("te", 15, 16 * ns, 16), -2.0, float(E), MUL, ADD, [("te", 0, E)], [("tj", 0, ns)])
            for k in range(nv):
                (v, r), (o, ro) = row(ns + k), own(ns + k)
                ts(V("cb", E * k, E * k + E), v, o, None, LT, None, r + ro, [("cb", k, k + 1)])
            for k in range(nv):
                ini, ri = (T.ti[:, ns + k:ns + k + 1], [("ti", ns, 28)]) if last else (-192.0, [])
                scan(V("sc", 224 * k, 224 * k + 224), V("cb", E * k, E * k + 224), V("cb", E * k + 224, E * k + E), ini, ADD, ADD,
                     ri + [("cb", k, k + 1)], [("sc", k, k + 1)])
            ts(V("pos", ns, 28), V("sc", 223, 224 * nv, 224), 192.0, None, ADD, None, [("sc", 0, nv)], [("pos", ns, 28)])
            if not last:
                ts(V("pos", 0, ns), V("acc", 0, ns), 0.5, 223.5, MUL, ADD, [("acc", 0, ns)], [("pos", 0, ns)])
            else:
                tt(V("posf", 0, ns), V("acc", 0, ns), V("tj", 0, ns), ADD, [("acc", 0, ns), ("tj", 0, ns)], [("posf", 0, ns)])
                ts(V("pos", 0, ns), V("posf", 0, ns), 0.5, None, MUL, None, [("posf", 0, ns)], [("pos", 0, ns)])
        tc(V("ordr", 0, E).indirect(V("pos", 0, 28)), V("iom", 0, E), [("iom", 0, E), ("pos", 0, 28)], [("ordr", 0, E)])
        wrap(V("ordr", 0, E), [("ordr", 0, E)], "b1", "b2")
        ts(V("ordl", 0, 28), V("b2", 15, E, 16), 192.0, None, ADD, None, [("b2", 0, E)], [("ordl", 0, 28)])
        for b in range(3):
            act(V("vs", E * b, E * b + E), V("vp", E * b, E * b + E).indirect(V("ordl", 0, 28)), COPY,
                [("vp%d" % b, 0, E), ("ordl", 0, 28)], [("vs%d" % b, 0, 1)])
        tc(V("vs", 3 * E, 4 * E), V("vp", 3 * E, 4 * E).indirect(V("ordl", 0, 28)), [("vp3", 0, E), ("ordl", 0, 28)], [("vs3", 0, 1)])
        if t == 1:
            scan(V("lr", 0, E), V("ios", 0, E), K, 0.0, MAX, SUB, [("ios", 0, E)] + KR, [("lr", 0, E)])
            act(V("s1", 0, E), V("lr", 0, E), IDEN, [("lr", 0, E)], [("s1", 0, E)], bias=0.5 - TOP[2] - CENTER, scale=-6562.0)
            act(V("s2", 0, E), V("lr", 4, E + 4), IDEN, [("lr", 0, E + 16)], [("s2", 0, E)], bias=1.0, scale=-2.0)
        if last:
            act(V("ks", 1, 1 + E), K.indirect(V("ordl", 0, 28)), COPY, KR + [("ordl", 0, 28)], [("ks", 1, 1 + E)])
        for b in (3, 0, 1, 2):
            o = E * b
            tt(V("mm", o + 1, o + E - 1), V("vs", o, o + E - 2), V("vs", o + 2, o + E), MAX, [("vs%d" % b, 0, 1)], [("mm%d" % b, 0, 1)])
        ends = [("vs%d" % b, 0, 1) for b in range(4)]
        tt(V("mm", 0, 4 * E, E), V("vs", 0, 4 * E, E), V("vs", 1, 4 * E, E), MAX, ends, [("mm%d" % b, 1, 2) for b in range(4)])
        tt(V("mm", E - 1, 4 * E, E), V("vs", E - 1, 4 * E, E), V("vs", E - 2, 4 * E, E), MAX, ends, [("mm%d" % b, 2, 3) for b in range(4)])

        def fused(b, lo, hi):
            tt(V("zt", 4 * lo + b, 4 * hi, 4), V("mm", E * b, E * b + E).indirect(V("pos", lo // 16, hi // 16)), V("vp", E * b + lo, E * b + hi), ADD,
               [("mm%d" % b, 0, 3), ("pos", 0, 28), ("vp%d" % b, lo, hi)], [("z%d" % b, lo, hi)])

        def product(lo, hi, b0):
            quant("qz", "sz", "zt", lo, hi, [("z%d" % b, lo, hi) for b in range(4)])
            for b in range(4):
                mx(b0 + b, hi - lo, "qw", "sw", 128 * b, "qz", "sz", lo, hi)

        xo, xn = "xt%d" % t, "xt%d" % (t + 1)

        def update(lo, hi, b0):
            for b in range(4):
                tt(V(xn, 4 * lo + b, 4 * hi, 4), bank(b0 + b, 0, hi - lo), V(xo, 4 * lo + b, 4 * hi, 4), ADD,
                   [("b%d" % (b0 + b), 0, 1), ("x%d_%d" % (t, b), lo, hi)], [("x%d_%d" % (t + 1, b), lo, hi)])

        def planes(lo, hi):
            for b in range(4):
                act(V("vp", E * b + lo, E * b + hi), V(xn, 4 * lo + b, 4 * hi, 4), COPY, [("x%d_%d" % (t + 1, b), lo, hi)], [("vp%d" % b, lo, hi)], scale=2.0 ** -6)

        qn, sn = "qx%d" % (t + 1), "sx%d" % (t + 1)
        cut = 256 if last else 128
        for b in (3, 0, 1, 2):
            fused(b, 0, cut)
        product(0, cut, 0)
        fused(0, cut, C)
        update(0, cut, 0)
        fused(1, cut, C)
        quant(qn, sn, xn, 0, cut, xr(t + 1, 0, cut))
        if not last:
            send(t + 1)
            mx(0, 128, "qur", "sur", 0, qn, sn, 0, 128)
            planes(0, 128)
        else:
            dma("s", "dca", [(qn, 0, cut)], [], T.oc[:, 0:4 * cut], V(qn, 0, cut).bitcast(dt.uint8))
            mx(0, cut, "qv", "sv", 0, qn, sn, 0, cut)
            act(V("yr", 0, cut), bank(0, 0, cut), COPY, [("b0", 0, 1)], [("yr", 0, cut)])
            dma("s", "dya", [("yr", 0, cut)], [], T.y[:, 0:cut], T.yr[:, 0:cut])
        fused(2, cut, C)
        fused(3, cut, C)
        product(cut, C, 4)
        if t == 0:
            scan(V("g1", 0, E), V("s2", 0, E), V("ga1", 0, E), 0.0, MAX, ADD, [("s2", 0, E), ("ga1", 0, E)], [("g1", 0, E)])
        elif t == 1:
            scan(V("g1", 0, E), V("s2", 0, E), V("s1", 0, E), 0.0, MAX, ADD, [("s1", 0, E), ("s2", 0, E)], [("g1", 0, E)])
        else:
            tt(V("eqs", 0, E), V("ks", 1, E + 1), V("ks", 0, E), EQ, [("ks", 0, E + 1)], [("eqs", 0, E)])
            scan(V("rr", 0, E), V("ones", 0, E), V("eqs", 0, E), 0.0, ADD, MUL, [("ones", 0, 512), ("eqs", 0, E)], [("rr", 0, E)])
            scan(V("lw", 0, E), V("iof", 0, E), V("rr", 0, E), 0.0, MAX, SUB, [("iof", 0, E), ("rr", 0, E)], [("lw", 0, E)])
        update(cut, C, 4)
        quant(qn, sn, xn, cut, C, xr(t + 1, cut, C))
        if not last:
            words(t + 1, 0, 0, 128, 0, 128)
            planes(128, C)
        else:
            act(V("lvr", 0, E), V("lw", 0, E).indirect(V("pos", 0, 28)), COPY, [("lw", 0, E), ("pos", 0, 28)], [("lvr", 0, E)])
            dma("s", "dlv", [("lvr", 0, E)], [], T.lv[:, :], T.lvr[0:128:16, 0:E])

    q, s = "qx%d" % NR, "sx%d" % NR
    mx(1, C - cut, "qv", "sv", 0, q, s, cut, C)
    dma("s", "dcb", [(q, cut, C)], [], T.oc[:, 4 * cut:4 * C], V(q, cut, C).bitcast(dt.uint8))
    for k in range(4):
        dma("s", "ds%d" % k, [(q, 0, C)], [], T.osc[4 * k:4 * k + 4, 0:C], T[s][32 * k:32 * k + 4, 0:C])
    act(V("yr", cut, C), bank(1, 0, C - cut), COPY, [("b1", 0, 1)], [("yr", cut, C)])
    dma("a", "dyb", [("yr", cut, C)], [], T.y[:, cut:C], T.yr[:, cut:C])
    for sem in count:
        g.wait_ge(T.sem[sem], count[sem])
    for sem in DMAS:
        g.wait_ge(T.sem[sem], 16)
    g.wait_ge(T.sem.left, 2 * NR * len(send_engines(core, prev)))
